import numpy as np
import ml_dtypes


def mxq(x, axis, fmt="e4m3"):
    dtype, down = {"e4m3": (ml_dtypes.float8_e4m3fn, 7), "e5m2": (ml_dtypes.float8_e5m2, 14)}[fmt]
    v = np.moveaxis(np.asarray(x, np.float32).astype(ml_dtypes.bfloat16).astype(np.float64), axis, -1)
    blocks = v.reshape(v.shape[:-1] + (-1, 32))
    amax = np.abs(blocks).max(-1, keepdims=True)
    byte = np.maximum(np.where(amax > 0, np.frexp(amax)[1] - 1 + 127, 0) - down, 1)
    scale = np.exp2(byte - 127.0)
    codes = (blocks / scale).astype(np.float32).astype(dtype).astype(np.float64)
    return np.moveaxis((codes * scale).reshape(v.shape), -1, axis)


WIDE = False


def mx_kscale(k):
    if not WIDE:
        return np.ones(k)
    levels = np.array([10, -10, 5, -5, 0])
    if k % 512:
        return np.exp2(np.random.permutation(np.resize(levels, k // 32))).repeat(32)
    a = np.empty((k // 512, 16))
    for p in range(k // 512):
        a[p, :8] = np.random.permutation(np.resize(levels, 8))
        for g in range(8):
            far = levels[np.abs(levels - a[p, g]) >= 10]
            a[p, g + 8] = far[np.random.randint(len(far))]
    return np.exp2(a.ravel()).repeat(32)


def f64(x):
    return np.asarray(x).astype(np.float64)


def striped(idx):
    return np.tile(np.asarray(idx).reshape(-1, 16).T, (8, 1)).astype(np.uint16)


def unstriped(offs):
    return offs[:16].T.reshape(-1).astype(np.int64)


E2M1 = np.array([0.0, 0.5, 1.0, 1.5, 2.0, 3.0, 4.0, 6.0, -0.0, -0.5, -1.0, -1.5, -2.0, -3.0, -4.0, -6.0])


def pack_weight(w, fmt):
    k, n = w.shape
    w = f64(np.asarray(w, np.float32).astype(ml_dtypes.bfloat16)).reshape(k // 32, 32, n)
    amax = np.abs(w).max(1)
    if fmt == "e4m3":
        byte = np.frexp(amax)[1] - 1 + 127 - 7
    else:
        mant, ex = np.frexp(amax / 6.0)
        byte = np.where(mant > 0.5, ex, ex - 1) + 127
    byte = np.clip(np.where(amax > 0, byte, 1), 1, 254)
    scaled = (w * np.exp2(127.0 - byte)[:, None, :]).reshape(k, n).astype(np.float32)
    by_word = np.ascontiguousarray(scaled.reshape(k // 512, 128, 4, n).transpose(0, 1, 3, 2))
    if fmt == "e4m3":
        words = by_word.astype(ml_dtypes.float8_e4m3fn).view(np.uint8)
    else:
        c = by_word.astype(ml_dtypes.float4_e2m1fn).view(np.uint8) & 0xF
        words = (c[..., 0::2] | (c[..., 1::2] << 4)).reshape(k // 512, 128, 2 * n)
    return np.ascontiguousarray(words), np.ascontiguousarray(byte.astype(np.uint8).reshape(k // 512, 16, n))


def unpack_weight(words, scales, fmt):
    g, _, n = scales.shape
    words = np.ascontiguousarray(words).reshape(g, 128, n, -1)
    if fmt == "e4m3":
        vals = words.view(ml_dtypes.float8_e4m3fn).astype(np.float64)
    else:
        nib = np.empty((g, 128, n, 4), np.uint8)
        nib[..., 0::2] = words & 0xF
        nib[..., 1::2] = words >> 4
        vals = E2M1[nib]
    vals = vals * np.repeat(np.exp2(scales.astype(np.float64) - 127.0), 8, axis=1)[..., None]
    return vals.transpose(0, 1, 3, 2).reshape(g * 512, n)


B, N, T, D, NQ = 1, 1024, 4096, 512, 128
SEG = 32


def setup_inputs():
    n = np.random.standard_normal
    pages = np.random.permutation(T // 32)[:B * N // 32]
    idx = (pages[:, None] * 32 + np.arange(32)[None, :]).reshape(-1)
    s = mx_kscale(D)[:, None]
    kp = pack_weight(n((D, T)) / s, "e4m3")
    return {
        "qT": (n((B, D, NQ)) * s * (1.00 / np.sqrt(D))).astype(np.float32),
        "k_words": kp[0],
        "k_scales": kp[1],
        "kb": np.tile(n(4096), (128, 1)).astype(np.float32),
        "im": (np.random.uniform(0.5, 2.5, (B, NQ, 1))).astype(np.float32),
        "offs": striped(idx),
    }


def reference(qT, k_words, k_scales, kb, im, offs):
    idx = unstriped(offs)
    pick = lambda x, which: x[:, which].reshape(x.shape[0], B, -1).transpose(1, 0, 2)
    k = unpack_weight(k_words, k_scales, "e4m3")
    kg = pick(k, idx)
    qq = mxq(f64(qT), 1, "e4m3")
    a = qq.transpose(0, 2, 1) @ kg
    y = np.maximum((a + pick(f64(kb), idx)[:, :1, :]).reshape(B, NQ, N // SEG, SEG).max(-1), f64(im))
    return y

@@ -1,0 +1,127 @@
+from contextlib import ExitStack
+
+import concourse.mybir as mybir
+from concourse.masks import make_identity
+
+F32 = mybir.dt.float32
+BF16 = mybir.dt.bfloat16
+I32 = mybir.dt.int32
+U32 = mybir.dt.uint32
+U16 = mybir.dt.uint16
+U8 = mybir.dt.uint8
+FP8X4 = mybir.dt.float8_e4m3fn_x4
+IDENTITY = mybir.ActivationFunctionType.Identity
+MAX = mybir.AluOpType.max
+AXIS_X = mybir.AxisListType.X
+
+P = 128
+PACK = 4
+T = 4096
+N = 1024
+NQ = 128
+SEG = 32
+HALF = N // 2
+TILES = N // P
+KB_ROW = P - 1
+
+FLOPS = 2 * 512 * NQ * N
+BYTES = P * T * 4 + 16 * T + 4 * T + 512 * NQ * 4 + NQ * 4 + P * 64 * 2 + NQ * 32 * 4
+
+
+def tile_attend_xtr_kernel(tc, qT, k_words, k_scales, kb, im, offs, out):
+    nc = tc.nc
+    with ExitStack() as ctx:
+        keep = ctx.enter_context(tc.tile_pool(name="keep", bufs=1))
+        psum = ctx.enter_context(tc.psum_pool(name="psum", bufs=1))
+
+        ident = keep.tile([P, P], F32, name="ident")
+        make_identity(nc, ident[:])
+
+        offsets = keep.tile([P, N // 16], U16, name="offsets")
+        nc.sync.dma_start(offsets[:], offs)
+        words = keep.tile([P, T], I32, name="words", align_bytes=64)
+        nc.sync.dma_start(words[:], k_words[0].rearrange("p n t -> p (n t)").bitcast(I32))
+
+        scales = keep.tile([P, T], U8, name="scales", align_bytes=64)
+        nc.vector.memset(scales[:].bitcast(I32), 0)
+        bias_row = keep.tile([P, T], F32, name="bias_row", align_bytes=64)
+        nc.scalar.dma_start(bias_row[KB_ROW:P, :], kb[0:1, :])
+        for quad in range(4):
+            nc.scalar.dma_start(
+                scales[32 * quad : 32 * quad + 4, :].bitcast(I32),
+                k_scales[0, 4 * quad : 4 * quad + 4, :].bitcast(I32),
+            )
+        nc.vector.memset(bias_row[0:KB_ROW, :], 0.0)
+
+        q_raw = keep.tile([P, PACK, NQ], F32, name="q_raw", tag="q_then_floor")
+        nc.scalar.dma_start(q_raw[:], qT[0].rearrange("(p j) w -> p j w", j=PACK))
+
+        bias_listed = keep.tile([P, N], F32, name="bias_listed", align_bytes=64)
+        nc.vector.tensor_copy(bias_listed[:], bias_row[:].indirect(offsets[:]))
+        bias_cols = keep.tile([P, TILES], F32, name="bias_cols")
+        for h in range(2):
+            turned = psum.tile([P, 4, P], F32, name="turned", tag="turn%d" % h)
+            for i in range(4):
+                c0 = (4 * h + i) * P
+                nc.tensor.transpose(turned[:, i, :], bias_listed[:, c0 : c0 + P], ident[:])
+            nc.scalar.activation(bias_cols[:, 4 * h : 4 * h + 4], turned[:, :, KB_ROW], IDENTITY)
+
+        q_grouped = keep.tile([P, NQ, PACK], BF16, name="q_grouped", align_bytes=64)
+        nc.scalar.copy(q_grouped[:], q_raw[:].rearrange("p j w -> p w j"))
+        floor = keep.tile([P, 1], F32, name="floor", tag="q_then_floor")
+        nc.sync.dma_start(floor[:], im[0])
+        q_codes = keep.tile([P, NQ], U32, name="q_codes", align_bytes=64)
+        q_scales = keep.tile([P, NQ], U8, name="q_scales", align_bytes=64)
+        nc.vector.quantize_mx(
+            out=q_codes[:].bitcast(FP8X4),
+            scales=q_scales[:],
+            in_=q_grouped[:].rearrange("p w j -> p (w j)"),
+        )
+
+        scales_listed = keep.tile([P, N], U8, name="scales_listed", align_bytes=64)
+        nc.vector.tensor_copy(scales_listed[:], scales[:].indirect(offsets[:]))
+
+        words_listed = []
+        for h in range(2):
+            w = keep.tile([P, HALF], U32, name="words_listed%d" % h, align_bytes=64)
+            cols = HALF // 16
+            nc.vector.tensor_copy(w[:], words[:].bitcast(U32).indirect(offsets[:, h * cols : (h + 1) * cols]))
+            words_listed.append(w)
+
+        best = keep.tile([P, N // SEG], F32, name="best")
+        score_banks = [(0, 1), (2, 3), (4,), (5,), (6,), (7,)]
+        score_tags = ["s0", "s1", "s2", "s3", "s4", "s0"]
+        back_groups = [(0, 1, 2, 3), (4, 5), (6, 7)]
+        back_tags = ["turn0", "turn1", "turn2"]
+        biased = {}
+        for tiles, tag in zip(score_banks, score_tags):
+            bank = psum.tile([P, len(tiles), NQ], F32, name="bank", tag=tag)
+            for i, t in enumerate(tiles):
+                c0 = (t % 4) * P
+                nc.tensor.matmul_mx(
+                    out=bank[:, i, :],
+                    lhsT=words_listed[t // 4][:, c0 : c0 + P].bitcast(FP8X4),
+                    lhsT_scale=scales_listed[:, t * P : (t + 1) * P],
+                    rhs=q_codes[:].bitcast(FP8X4),
+                    rhs_scale=q_scales[:],
+                    start=True,
+                    stop=True,
+                )
+            for i, t in enumerate(tiles):
+                b = keep.tile([P, NQ], F32, name="biased%d" % t)
+                nc.scalar.activation(b[:], bank[:, i, :], IDENTITY, bias=bias_cols[:, t : t + 1])
+                biased[t] = b
+            for group, back_tag in zip(back_groups, back_tags):
+                if group[-1] == tiles[-1]:
+                    back = psum.tile([P, len(group), P], F32, name="back", tag=back_tag)
+                    for i, t in enumerate(group):
+                        nc.tensor.transpose(back[:, i, :], biased[t][:], ident[:])
+                    j0 = group[0] * P // SEG
+                    j1 = (group[-1] + 1) * P // SEG
+                    nc.vector.tensor_reduce(
+                        best[:, j0:j1], back[:].rearrange("p i (j s) -> p (i j) s", s=SEG), AXIS_X, MAX
+                    )
+
+        result = keep.tile([P, N // SEG], F32, name="result")
+        nc.vector.tensor_scalar(result[:], best[:], floor[:], None, MAX)
+        nc.sync.dma_start(out[0], result[:])

@@ -1,7 +1,6 @@
 from contextlib import ExitStack
 
 import concourse.mybir as mybir
-from concourse.masks import make_identity
 
 F32 = mybir.dt.float32
 BF16 = mybir.dt.bfloat16
@@ -11,7 +10,12 @@ U16 = mybir.dt.uint16
 U8 = mybir.dt.uint8
 FP8X4 = mybir.dt.float8_e4m3fn_x4
 IDENTITY = mybir.ActivationFunctionType.Identity
+ABS = mybir.ActivationFunctionType.Abs
+RELU = mybir.ActivationFunctionType.Relu
 MAX = mybir.AluOpType.max
+ADD = mybir.AluOpType.add
+MULT = mybir.AluOpType.mult
+IS_EQUAL = mybir.AluOpType.is_equal
 AXIS_X = mybir.AxisListType.X
 
 P = 128
@@ -32,42 +36,43 @@ def tile_attend_xtr_kernel(tc, qT, k_words, k_scales, kb, im, offs, out):
     nc = tc.nc
     with ExitStack() as ctx:
         keep = ctx.enter_context(tc.tile_pool(name="keep", bufs=1))
+        shared = ctx.enter_context(tc.tile_pool(name="shared", bufs=1))
         psum = ctx.enter_context(tc.psum_pool(name="psum", bufs=1))
 
-        ident = keep.tile([P, P], F32, name="ident")
-        make_identity(nc, ident[:])
-
+        q_raw = keep.tile([P, PACK, NQ], F32, name="q_raw", tag="q_then_floor")
+        nc.sync.dma_start(q_raw[:], qT[0].rearrange("(p j) w -> p j w", j=PACK))
         offsets = keep.tile([P, N // 16], U16, name="offsets")
         nc.sync.dma_start(offsets[:], offs)
+        bias_row = keep.tile([P, T], F32, name="bias_row", align_bytes=64)
+        nc.sync.dma_start(bias_row[KB_ROW:P, :], kb[0:1, :])
+
         words = keep.tile([P, T], I32, name="words", align_bytes=64)
-        nc.sync.dma_start(words[:], k_words[0].rearrange("p n t -> p (n t)").bitcast(I32))
+        words_hbm = k_words[0].rearrange("p n t -> p (n t)").bitcast(I32)
+        nc.sync.dma_start(words[:, 0:1024], words_hbm[:, 0:1024])
 
         scales = keep.tile([P, T], U8, name="scales", align_bytes=64)
-        nc.vector.memset(scales[:].bitcast(I32), 0)
-        bias_row = keep.tile([P, T], F32, name="bias_row", align_bytes=64)
-        nc.scalar.dma_start(bias_row[KB_ROW:P, :], kb[0:1, :])
+        scale_words = scales[:].bitcast(I32)
+        nc.gpsimd.memset(scale_words[:, 512:1024], 0)
+        nc.vector.memset(scale_words[:, 0:255], 0)
+        nc.vector.memset(scale_words[:, 255:512], 0)
         for quad in range(4):
-            nc.scalar.dma_start(
+            nc.sync.dma_start(
                 scales[32 * quad : 32 * quad + 4, :].bitcast(I32),
                 k_scales[0, 4 * quad : 4 * quad + 4, :].bitcast(I32),
             )
-        nc.vector.memset(bias_row[0:KB_ROW, :], 0.0)
+        nc.sync.dma_start(words[:, 1024:T], words_hbm[:, 1024:T])
 
-        q_raw = keep.tile([P, PACK, NQ], F32, name="q_raw", tag="q_then_floor")
-        nc.scalar.dma_start(q_raw[:], qT[0].rearrange("(p j) w -> p j w", j=PACK))
+        diagonal = keep.tile([P, P], F32, name="diagonal")
+        nc.gpsimd.iota(diagonal[:], [[1, P]], base=0, channel_multiplier=-1, allow_small_or_imprecise_dtypes=True)
 
-        bias_listed = keep.tile([P, N], F32, name="bias_listed", align_bytes=64)
-        nc.vector.tensor_copy(bias_listed[:], bias_row[:].indirect(offsets[:]))
-        bias_cols = keep.tile([P, TILES], F32, name="bias_cols")
-        for h in range(2):
-            turned = psum.tile([P, 4, P], F32, name="turned", tag="turn%d" % h)
-            for i in range(4):
-                c0 = (4 * h + i) * P
-                nc.tensor.transpose(turned[:, i, :], bias_listed[:, c0 : c0 + P], ident[:])
-            nc.scalar.activation(bias_cols[:, 4 * h : 4 * h + 4], turned[:, :, KB_ROW], IDENTITY)
+        bias_words = bias_row[0:KB_ROW, :].bitcast(I32)
+        nc.vector.memset(bias_words[:, 0:1151], 0)
+        nc.vector.memset(bias_words[:, 1151:2304], 0)
+        nc.gpsimd.memset(bias_words[:, 2304:T], 0)
 
-        q_grouped = keep.tile([P, NQ, PACK], BF16, name="q_grouped", align_bytes=64)
-        nc.scalar.copy(q_grouped[:], q_raw[:].rearrange("p j w -> p w j"))
+        staging = shared.tile([P, 9 * N // 2], BF16, name="staging", align_bytes=64, offset=0)
+        q_grouped = staging[:, 0 : NQ * PACK]
+        nc.scalar.copy(q_grouped.rearrange("p (w j) -> p w j", j=PACK), q_raw[:].rearrange("p j w -> p w j"))
         floor = keep.tile([P, 1], F32, name="floor", tag="q_then_floor")
         nc.sync.dma_start(floor[:], im[0])
         q_codes = keep.tile([P, NQ], U32, name="q_codes", align_bytes=64)
@@ -75,53 +80,102 @@ def tile_attend_xtr_kernel(tc, qT, k_words, k_scales, kb, im, offs, out):
         nc.vector.quantize_mx(
             out=q_codes[:].bitcast(FP8X4),
             scales=q_scales[:],
-            in_=q_grouped[:].rearrange("p w j -> p (w j)"),
+            in_=q_grouped,
         )
 
-        scales_listed = keep.tile([P, N], U8, name="scales_listed", align_bytes=64)
+        ident = keep.tile([P, P], F32, name="ident")
+        distance = keep.tile([P, P], F32, name="distance")
+        nc.scalar.activation(distance[:], diagonal[:], ABS)
+        nc.scalar.activation(ident[:], distance[:], RELU, bias=1.0, scale=-1.0)
+
+        bias_listed = shared.tile([P, N], F32, name="bias_listed", align_bytes=64, offset=0)
+        nc.vector.tensor_copy(bias_listed[:], bias_row[:].indirect(offsets[:]))
+        bias_cols = keep.tile([P, TILES], F32, name="bias_cols")
+        for h in range(2):
+            turned = psum.tile([P, 4, P], F32, name="turned", tag="b%d" % h)
+            for i in range(4):
+                c0 = (4 * h + i) * P
+                nc.tensor.transpose(turned[:, i, :], bias_listed[:, c0 : c0 + P], ident[:])
+            nc.scalar.activation(bias_cols[:, 4 * h : 4 * h + 4], turned[:, :, KB_ROW], IDENTITY)
+
+        groups = (("Q",0,4,("s0",),"b2",),("Q",4,4,("s1",),"b3",),)
+        bias_wide = {}
+        for path, t0, nt, bank_tags, back_tag in groups:
+            if path == "Q":
+                spread = psum.tile([P, nt, P], F32, name="spread", tag=back_tag)
+                for i in range(nt):
+                    nc.tensor.transpose(
+                        spread[:, i, :], bias_cols[:, t0 + i : t0 + i + 1].to_broadcast([P, P]), ident[:]
+                    )
+                wide = keep.tile([P, nt * P], F32, name="bias_wide%d" % t0)
+                nc.scalar.copy(wide[:], spread[:].rearrange("p i n -> p (i n)"))
+                bias_wide[t0] = wide
+
+        scales_listed = shared.tile([P, N], U8, name="scales_listed", align_bytes=64, offset=4 * N)
         nc.vector.tensor_copy(scales_listed[:], scales[:].indirect(offsets[:]))
 
+        words_all = shared.tile([P, N], U32, name="words_all", align_bytes=64, offset=5 * N)
         words_listed = []
         for h in range(2):
-            w = keep.tile([P, HALF], U32, name="words_listed%d" % h, align_bytes=64)
+            w = words_all[:, h * HALF : (h + 1) * HALF]
             cols = HALF // 16
-            nc.vector.tensor_copy(w[:], words[:].bitcast(U32).indirect(offsets[:, h * cols : (h + 1) * cols]))
+            nc.vector.tensor_copy(w, words[:].bitcast(U32).indirect(offsets[:, h * cols : (h + 1) * cols]))
             words_listed.append(w)
 
         best = keep.tile([P, N // SEG], F32, name="best")
-        score_banks = [(0, 1), (2, 3), (4,), (5,), (6,), (7,)]
-        score_tags = ["s0", "s1", "s2", "s3", "s4", "s0"]
-        back_groups = [(0, 1, 2, 3), (4, 5), (6, 7)]
-        back_tags = ["turn0", "turn1", "turn2"]
-        biased = {}
-        for tiles, tag in zip(score_banks, score_tags):
-            bank = psum.tile([P, len(tiles), NQ], F32, name="bank", tag=tag)
-            for i, t in enumerate(tiles):
-                c0 = (t % 4) * P
+        pending = []
+        for path, t0, nt, bank_tags, back_tag in groups:
+            j0 = t0 * P // SEG
+            j1 = (t0 + nt) * P // SEG
+            if path == "Q":
+                bank = psum.tile([P, nt * P], F32, name="bank", tag=bank_tags[0])
+                c0 = (t0 % 4) * P
                 nc.tensor.matmul_mx(
-                    out=bank[:, i, :],
-                    lhsT=words_listed[t // 4][:, c0 : c0 + P].bitcast(FP8X4),
-                    lhsT_scale=scales_listed[:, t * P : (t + 1) * P],
-                    rhs=q_codes[:].bitcast(FP8X4),
-                    rhs_scale=q_scales[:],
+                    out=bank[:],
+                    lhsT=q_codes[:].bitcast(FP8X4),
+                    lhsT_scale=q_scales[:],
+                    rhs=words_listed[t0 // 4][:, c0 : c0 + nt * P].bitcast(FP8X4),
+                    rhs_scale=scales_listed[:, t0 * P : (t0 + nt) * P],
                     start=True,
                     stop=True,
                 )
-            for i, t in enumerate(tiles):
-                b = keep.tile([P, NQ], F32, name="biased%d" % t)
-                nc.scalar.activation(b[:], bank[:, i, :], IDENTITY, bias=bias_cols[:, t : t + 1])
-                biased[t] = b
-            for group, back_tag in zip(back_groups, back_tags):
-                if group[-1] == tiles[-1]:
-                    back = psum.tile([P, len(group), P], F32, name="back", tag=back_tag)
-                    for i, t in enumerate(group):
-                        nc.tensor.transpose(back[:, i, :], biased[t][:], ident[:])
-                    j0 = group[0] * P // SEG
-                    j1 = (group[-1] + 1) * P // SEG
-                    nc.vector.tensor_reduce(
-                        best[:, j0:j1], back[:].rearrange("p i (j s) -> p (i j) s", s=SEG), AXIS_X, MAX
-                    )
+                summed = keep.tile([P, j1 - j0, SEG + 4], F32, name="summed%d" % t0)
+                nc.scalar.copy(summed[:, :, SEG], floor[:].to_broadcast([P, j1 - j0]))
+                nc.vector.tensor_tensor(
+                    summed[:, :, 0:SEG],
+                    bank[:].rearrange("p (j s) -> p j s", s=SEG),
+                    bias_wide[t0][:].rearrange("p (j s) -> p j s", s=SEG),
+                    ADD,
+                )
+                pending.append((j0, j1, summed[:, :, 0 : SEG + 1]))
+            else:
+                per_bank = nt // len(bank_tags)
+                biased = []
+                for k, tag in enumerate(bank_tags):
+                    bank = psum.tile([P, per_bank, NQ], F32, name="bank", tag=tag)
+                    for i in range(per_bank):
+                        t = t0 + k * per_bank + i
+                        c0 = (t % 4) * P
+                        nc.tensor.matmul_mx(
+                            out=bank[:, i, :],
+                            lhsT=words_listed[t // 4][:, c0 : c0 + P].bitcast(FP8X4),
+                            lhsT_scale=scales_listed[:, t * P : (t + 1) * P],
+                            rhs=q_codes[:].bitcast(FP8X4),
+                            rhs_scale=q_scales[:],
+                            start=True,
+                            stop=True,
+                        )
+                    for i in range(per_bank):
+                        t = t0 + k * per_bank + i
+                        b = keep.tile([P, NQ], F32, name="biased%d" % t)
+                        nc.scalar.activation(b[:], bank[:, i, :], IDENTITY, bias=bias_cols[:, t : t + 1])
+                        biased.append(b)
+                back = psum.tile([P, nt, P], F32, name="back", tag=back_tag)
+                for i in range(nt):
+                    nc.tensor.transpose(back[:, i, :], biased[i][:], ident[:])
+                pending.append((j0, j1, back[:].rearrange("p i (j s) -> p (i j) s", s=SEG)))
+        for k in [0,1]:
+            j0, j1, source = pending[k]
+            nc.vector.tensor_reduce(best[:, j0:j1], source, AXIS_X, MAX)
 
-        result = keep.tile([P, N // SEG], F32, name="result")
-        nc.vector.tensor_scalar(result[:], best[:], floor[:], None, MAX)
-        nc.sync.dma_start(out[0], result[:])
+        nc.sync.dma_start(out[0], best[:])

@@ -14,8 +14,6 @@ ABS = mybir.ActivationFunctionType.Abs
 RELU = mybir.ActivationFunctionType.Relu
 MAX = mybir.AluOpType.max
 ADD = mybir.AluOpType.add
-MULT = mybir.AluOpType.mult
-IS_EQUAL = mybir.AluOpType.is_equal
 AXIS_X = mybir.AxisListType.X
 
 P = 128
@@ -39,143 +37,108 @@ def tile_attend_xtr_kernel(tc, qT, k_words, k_scales, kb, im, offs, out):
         shared = ctx.enter_context(tc.tile_pool(name="shared", bufs=1))
         psum = ctx.enter_context(tc.psum_pool(name="psum", bufs=1))
 
-        q_raw = keep.tile([P, PACK, NQ], F32, name="q_raw", tag="q_then_floor")
-        nc.sync.dma_start(q_raw[:], qT[0].rearrange("(p j) w -> p j w", j=PACK))
+        at_scales = 0
+        at_q_grouped = 5 * 1024
+        at_bias_row = 6 * 1024
+        at_q_raw = at_bias_row + 4 * T
+
         offsets = keep.tile([P, N // 16], U16, name="offsets")
         nc.sync.dma_start(offsets[:], offs)
-        bias_row = keep.tile([P, T], F32, name="bias_row", align_bytes=64)
-        nc.sync.dma_start(bias_row[KB_ROW:P, :], kb[0:1, :])
-
-        words = keep.tile([P, T], I32, name="words", align_bytes=64)
-        words_hbm = k_words[0].rearrange("p n t -> p (n t)").bitcast(I32)
-        nc.sync.dma_start(words[:, 0:1024], words_hbm[:, 0:1024])
-
-        scales = keep.tile([P, T], U8, name="scales", align_bytes=64)
+        scales = shared.tile([P, T], U8, name="scales", align_bytes=64, offset=at_scales)
         scale_words = scales[:].bitcast(I32)
-        nc.gpsimd.memset(scale_words[:, 512:1024], 0)
-        nc.vector.memset(scale_words[:, 0:255], 0)
-        nc.vector.memset(scale_words[:, 255:512], 0)
-        for quad in range(4):
-            nc.sync.dma_start(
-                scales[32 * quad : 32 * quad + 4, :].bitcast(I32),
-                k_scales[0, 4 * quad : 4 * quad + 4, :].bitcast(I32),
-            )
-        nc.sync.dma_start(words[:, 1024:T], words_hbm[:, 1024:T])
+        nc.sync.dma_start(scale_words[48:64, :], k_scales[0].bitcast(I32))
+        q_raw = shared.tile([P, PACK, NQ], F32, name="q_raw", align_bytes=64, offset=at_q_raw)
+        nc.sync.dma_start(q_raw[:], qT[0].rearrange("(p j) w -> p j w", j=PACK))
+        bias_row = shared.tile([P, T], F32, name="bias_row", align_bytes=64, offset=at_bias_row)
+        nc.sync.dma_start(bias_row[KB_ROW:P, :], kb[0:1, :])
+        words = keep.tile([P, T], I32, name="words", align_bytes=64)
+        nc.sync.dma_start(words[:], k_words[0].rearrange("p n t -> p (n t)").bitcast(I32))
+        floor = keep.tile([P, 1], F32, name="floor")
+        nc.sync.dma_start(floor[:], im[0])
+
+        nc.gpsimd.memset(scale_words[64:P, :], 0)
+        nc.vector.memset(scale_words[0:48, 0:511], 0)
+        nc.vector.memset(scale_words[0:48, 511:1024], 0)
+
+        bias_words = bias_row[0:KB_ROW, :].bitcast(I32)
+        nc.vector.memset(bias_words[:, 0:447], 0)
+        nc.vector.memset(bias_words[:, 447:896], 0)
+        nc.gpsimd.memset(bias_words[:, 896:T], 0)
 
         diagonal = keep.tile([P, P], F32, name="diagonal")
         nc.gpsimd.iota(diagonal[:], [[1, P]], base=0, channel_multiplier=-1, allow_small_or_imprecise_dtypes=True)
 
-        bias_words = bias_row[0:KB_ROW, :].bitcast(I32)
-        nc.vector.memset(bias_words[:, 0:1151], 0)
-        nc.vector.memset(bias_words[:, 1151:2304], 0)
-        nc.gpsimd.memset(bias_words[:, 2304:T], 0)
-
-        staging = shared.tile([P, 9 * N // 2], BF16, name="staging", align_bytes=64, offset=0)
-        q_grouped = staging[:, 0 : NQ * PACK]
-        nc.scalar.copy(q_grouped.rearrange("p (w j) -> p w j", j=PACK), q_raw[:].rearrange("p j w -> p w j"))
-        floor = keep.tile([P, 1], F32, name="floor", tag="q_then_floor")
-        nc.sync.dma_start(floor[:], im[0])
-        q_codes = keep.tile([P, NQ], U32, name="q_codes", align_bytes=64)
-        q_scales = keep.tile([P, NQ], U8, name="q_scales", align_bytes=64)
-        nc.vector.quantize_mx(
-            out=q_codes[:].bitcast(FP8X4),
-            scales=q_scales[:],
-            in_=q_grouped,
-        )
+        q_grouped = shared.tile([P, NQ * PACK], BF16, name="q_grouped", align_bytes=64, offset=at_q_grouped)
+        nc.scalar.copy(q_grouped[:].rearrange("p (w j) -> p w j", j=PACK), q_raw[:].rearrange("p j w -> p w j"))
 
         ident = keep.tile([P, P], F32, name="ident")
         distance = keep.tile([P, P], F32, name="distance")
         nc.scalar.activation(distance[:], diagonal[:], ABS)
         nc.scalar.activation(ident[:], distance[:], RELU, bias=1.0, scale=-1.0)
 
-        bias_listed = shared.tile([P, N], F32, name="bias_listed", align_bytes=64, offset=0)
-        nc.vector.tensor_copy(bias_listed[:], bias_row[:].indirect(offsets[:]))
-        bias_cols = keep.tile([P, TILES], F32, name="bias_cols")
-        for h in range(2):
-            turned = psum.tile([P, 4, P], F32, name="turned", tag="b%d" % h)
-            for i in range(4):
-                c0 = (4 * h + i) * P
-                nc.tensor.transpose(turned[:, i, :], bias_listed[:, c0 : c0 + P], ident[:])
-            nc.scalar.activation(bias_cols[:, 4 * h : 4 * h + 4], turned[:, :, KB_ROW], IDENTITY)
-
-        groups = (("Q",0,4,("s0",),"b2",),("Q",4,4,("s1",),"b3",),)
-        bias_wide = {}
-        for path, t0, nt, bank_tags, back_tag in groups:
-            if path == "Q":
-                spread = psum.tile([P, nt, P], F32, name="spread", tag=back_tag)
-                for i in range(nt):
-                    nc.tensor.transpose(
-                        spread[:, i, :], bias_cols[:, t0 + i : t0 + i + 1].to_broadcast([P, P]), ident[:]
-                    )
-                wide = keep.tile([P, nt * P], F32, name="bias_wide%d" % t0)
-                nc.scalar.copy(wide[:], spread[:].rearrange("p i n -> p (i n)"))
-                bias_wide[t0] = wide
-
-        scales_listed = shared.tile([P, N], U8, name="scales_listed", align_bytes=64, offset=4 * N)
+        scales_listed = keep.tile([P, N], U8, name="scales_listed", align_bytes=64)
         nc.vector.tensor_copy(scales_listed[:], scales[:].indirect(offsets[:]))
 
-        words_all = shared.tile([P, N], U32, name="words_all", align_bytes=64, offset=5 * N)
-        words_listed = []
+        plane = shared.tile([P, N], U8, name="plane", align_bytes=64, offset=at_q_raw)
+        nc.gpsimd.memset(plane[:].bitcast(I32), 0)
+        for r in range(4):
+            nc.scalar.dma_start(plane[r:P:32, :].bitcast(I32), scales_listed[48 + r : 64 : 4, :].bitcast(I32))
+
+        q_codes = shared.tile([P, NQ], U32, name="q_codes", align_bytes=64, offset=at_scales + 2048)
+        q_scales = keep.tile([P, NQ], U8, name="q_scales", align_bytes=64)
+        nc.vector.quantize_mx(out=q_codes[:].bitcast(FP8X4), scales=q_scales[:], in_=q_grouped[:])
+
+        cols = HALF // 16
+        bias_cols = keep.tile([P, TILES], F32, name="bias_cols")
+        bias_wide = []
         for h in range(2):
-            w = words_all[:, h * HALF : (h + 1) * HALF]
-            cols = HALF // 16
-            nc.vector.tensor_copy(w, words[:].bitcast(U32).indirect(offsets[:, h * cols : (h + 1) * cols]))
-            words_listed.append(w)
+            bias_listed = shared.tile(
+                [P, HALF], F32, name="bias_listed%d" % h, align_bytes=64, offset=at_scales + 2560 * h
+            )
+            nc.vector.tensor_copy(bias_listed[:], bias_row[:].indirect(offsets[:, h * cols : (h + 1) * cols]))
+            turned = psum.tile([P, 4, P], F32, name="turned", tag="b%d" % h)
+            for i in range(4):
+                nc.tensor.transpose(turned[:, i, :], bias_listed[:, i * P : (i + 1) * P], ident[:])
+            nc.scalar.activation(bias_cols[:, 4 * h : 4 * h + 4], turned[:, :, KB_ROW], IDENTITY)
+            spread = psum.tile([P, 4, P], F32, name="spread", tag="b%d" % (2 + h))
+            for i in range(4):
+                t = 4 * h + i
+                nc.tensor.transpose(spread[:, i, :], bias_cols[:, t : t + 1].to_broadcast([P, P]), ident[:])
+            wide = keep.tile([P, HALF], F32, name="bias_wide%d" % h)
+            nc.scalar.copy(wide[:], spread[:].rearrange("p i n -> p (i n)"))
+            bias_wide.append(wide)
+
+        words_listed = shared.tile([P, N], U32, name="words_listed", align_bytes=64, offset=at_q_grouped)
+        for h in range(2):
+            nc.vector.tensor_copy(
+                words_listed[:, h * HALF : (h + 1) * HALF],
+                words[:].bitcast(U32).indirect(offsets[:, h * cols : (h + 1) * cols]),
+            )
 
         best = keep.tile([P, N // SEG], F32, name="best")
-        pending = []
-        for path, t0, nt, bank_tags, back_tag in groups:
-            j0 = t0 * P // SEG
-            j1 = (t0 + nt) * P // SEG
-            if path == "Q":
-                bank = psum.tile([P, nt * P], F32, name="bank", tag=bank_tags[0])
-                c0 = (t0 % 4) * P
-                nc.tensor.matmul_mx(
-                    out=bank[:],
-                    lhsT=q_codes[:].bitcast(FP8X4),
-                    lhsT_scale=q_scales[:],
-                    rhs=words_listed[t0 // 4][:, c0 : c0 + nt * P].bitcast(FP8X4),
-                    rhs_scale=scales_listed[:, t0 * P : (t0 + nt) * P],
-                    start=True,
-                    stop=True,
-                )
-                summed = keep.tile([P, j1 - j0, SEG + 4], F32, name="summed%d" % t0)
-                nc.scalar.copy(summed[:, :, SEG], floor[:].to_broadcast([P, j1 - j0]))
-                nc.vector.tensor_tensor(
-                    summed[:, :, 0:SEG],
-                    bank[:].rearrange("p (j s) -> p j s", s=SEG),
-                    bias_wide[t0][:].rearrange("p (j s) -> p j s", s=SEG),
-                    ADD,
-                )
-                pending.append((j0, j1, summed[:, :, 0 : SEG + 1]))
-            else:
-                per_bank = nt // len(bank_tags)
-                biased = []
-                for k, tag in enumerate(bank_tags):
-                    bank = psum.tile([P, per_bank, NQ], F32, name="bank", tag=tag)
-                    for i in range(per_bank):
-                        t = t0 + k * per_bank + i
-                        c0 = (t % 4) * P
-                        nc.tensor.matmul_mx(
-                            out=bank[:, i, :],
-                            lhsT=words_listed[t // 4][:, c0 : c0 + P].bitcast(FP8X4),
-                            lhsT_scale=scales_listed[:, t * P : (t + 1) * P],
-                            rhs=q_codes[:].bitcast(FP8X4),
-                            rhs_scale=q_scales[:],
-                            start=True,
-                            stop=True,
-                        )
-                    for i in range(per_bank):
-                        t = t0 + k * per_bank + i
-                        b = keep.tile([P, NQ], F32, name="biased%d" % t)
-                        nc.scalar.activation(b[:], bank[:, i, :], IDENTITY, bias=bias_cols[:, t : t + 1])
-                        biased.append(b)
-                back = psum.tile([P, nt, P], F32, name="back", tag=back_tag)
-                for i in range(nt):
-                    nc.tensor.transpose(back[:, i, :], biased[i][:], ident[:])
-                pending.append((j0, j1, back[:].rearrange("p i (j s) -> p (i j) s", s=SEG)))
-        for k in [0,1]:
-            j0, j1, source = pending[k]
-            nc.vector.tensor_reduce(best[:, j0:j1], source, AXIS_X, MAX)
+        runs = HALF // SEG
+        sums = []
+        for h in range(2):
+            bank = psum.tile([P, HALF], F32, name="bank", tag="s%d" % h)
+            nc.tensor.matmul_mx(
+                out=bank[:],
+                lhsT=q_codes[:].bitcast(FP8X4),
+                lhsT_scale=q_scales[:],
+                rhs=words_listed[:, h * HALF : (h + 1) * HALF].bitcast(FP8X4),
+                rhs_scale=plane[:, h * HALF : (h + 1) * HALF],
+                start=True,
+                stop=True,
+            )
+            summed = keep.tile([P, runs, SEG + 4], F32, name="summed%d" % h)
+            nc.scalar.copy(summed[:, :, SEG], floor[:].to_broadcast([P, runs]))
+            nc.vector.tensor_tensor(
+                summed[:, :, 0:SEG],
+                bank[:].rearrange("p (j s) -> p j s", s=SEG),
+                bias_wide[h][:].rearrange("p (j s) -> p j s", s=SEG),
+                ADD,
+            )
+            sums.append(summed)
+        for h in range(2):
+            nc.vector.tensor_reduce(best[:, h * runs : (h + 1) * runs], sums[h][:, :, 0 : SEG + 1], AXIS_X, MAX)
 
         nc.sync.dma_start(out[0], best[:])

@@ -44,29 +44,29 @@ def tile_attend_xtr_kernel(tc, qT, k_words, k_scales, kb, im, offs, out):
 
         offsets = keep.tile([P, N // 16], U16, name="offsets")
         nc.sync.dma_start(offsets[:], offs)
-        scales = shared.tile([P, T], U8, name="scales", align_bytes=64, offset=at_scales)
-        scale_words = scales[:].bitcast(I32)
-        nc.sync.dma_start(scale_words[48:64, :], k_scales[0].bitcast(I32))
         q_raw = shared.tile([P, PACK, NQ], F32, name="q_raw", align_bytes=64, offset=at_q_raw)
         nc.sync.dma_start(q_raw[:], qT[0].rearrange("(p j) w -> p j w", j=PACK))
         bias_row = shared.tile([P, T], F32, name="bias_row", align_bytes=64, offset=at_bias_row)
         nc.sync.dma_start(bias_row[KB_ROW:P, :], kb[0:1, :])
+
+        scales = shared.tile([P, T], U8, name="scales", align_bytes=64, offset=at_scales)
+        scale_words = scales[:].bitcast(I32)
+        nc.gpsimd.memset(scale_words[:, 512:1024], 0)
+        nc.vector.memset(scale_words[:, 0:255], 0)
+        nc.vector.memset(scale_words[:, 255:512], 0)
+        nc.sync.dma_start(scale_words[0:P:8, :], k_scales[0].bitcast(I32))
         words = keep.tile([P, T], I32, name="words", align_bytes=64)
         nc.sync.dma_start(words[:], k_words[0].rearrange("p n t -> p (n t)").bitcast(I32))
         floor = keep.tile([P, 1], F32, name="floor")
         nc.sync.dma_start(floor[:], im[0])
 
-        nc.gpsimd.memset(scale_words[64:P, :], 0)
-        nc.vector.memset(scale_words[0:48, 0:511], 0)
-        nc.vector.memset(scale_words[0:48, 511:1024], 0)
-
-        bias_words = bias_row[0:KB_ROW, :].bitcast(I32)
-        nc.vector.memset(bias_words[:, 0:447], 0)
-        nc.vector.memset(bias_words[:, 447:896], 0)
-        nc.gpsimd.memset(bias_words[:, 896:T], 0)
-
         diagonal = keep.tile([P, P], F32, name="diagonal")
         nc.gpsimd.iota(diagonal[:], [[1, P]], base=0, channel_multiplier=-1, allow_small_or_imprecise_dtypes=True)
+
+        bias_words = bias_row[0:KB_ROW, :].bitcast(I32)
+        nc.vector.memset(bias_words[:, 0:1023], 0)
+        nc.vector.memset(bias_words[:, 1023:2048], 0)
+        nc.gpsimd.memset(bias_words[:, 2048:T], 0)
 
         q_grouped = shared.tile([P, NQ * PACK], BF16, name="q_grouped", align_bytes=64, offset=at_q_grouped)
         nc.scalar.copy(q_grouped[:].rearrange("p (w j) -> p w j", j=PACK), q_raw[:].rearrange("p j w -> p w j"))
@@ -82,9 +82,9 @@ def tile_attend_xtr_kernel(tc, qT, k_words, k_scales, kb, im, offs, out):
         plane = shared.tile([P, N], U8, name="plane", align_bytes=64, offset=at_q_raw)
         nc.gpsimd.memset(plane[:].bitcast(I32), 0)
         for r in range(4):
-            nc.scalar.dma_start(plane[r:P:32, :].bitcast(I32), scales_listed[48 + r : 64 : 4, :].bitcast(I32))
+            nc.scalar.dma_start(plane[r:P:32, :].bitcast(I32), scales_listed[8 * r : P : 32, :].bitcast(I32))
 
-        q_codes = shared.tile([P, NQ], U32, name="q_codes", align_bytes=64, offset=at_scales + 2048)
+        q_codes = shared.tile([P, NQ], U32, name="q_codes", align_bytes=64, offset=at_bias_row + 8192)
         q_scales = keep.tile([P, NQ], U8, name="q_scales", align_bytes=64)
         nc.vector.quantize_mx(out=q_codes[:].bitcast(FP8X4), scales=q_scales[:], in_=q_grouped[:])
 
@@ -116,29 +116,39 @@ def tile_attend_xtr_kernel(tc, qT, k_words, k_scales, kb, im, offs, out):
             )
 
         best = keep.tile([P, N // SEG], F32, name="best")
-        runs = HALF // SEG
-        sums = []
-        for h in range(2):
-            bank = psum.tile([P, HALF], F32, name="bank", tag="s%d" % h)
+        pieces = ((0, HALF), (HALF, HALF // 2), (HALF + HALF // 2, HALF // 2))
+
+        def add_biases(k):
+            c0, width = pieces[k]
+            bank = psum.tile([P, width], F32, name="bank", tag="s%d" % k)
             nc.tensor.matmul_mx(
                 out=bank[:],
                 lhsT=q_codes[:].bitcast(FP8X4),
                 lhsT_scale=q_scales[:],
-                rhs=words_listed[:, h * HALF : (h + 1) * HALF].bitcast(FP8X4),
-                rhs_scale=plane[:, h * HALF : (h + 1) * HALF],
+                rhs=words_listed[:, c0 : c0 + width].bitcast(FP8X4),
+                rhs_scale=plane[:, c0 : c0 + width],
                 start=True,
                 stop=True,
             )
-            summed = keep.tile([P, runs, SEG + 4], F32, name="summed%d" % h)
-            nc.scalar.copy(summed[:, :, SEG], floor[:].to_broadcast([P, runs]))
+            summed = keep.tile([P, width // SEG, SEG + 4], F32, name="summed%d" % k)
+            nc.scalar.copy(summed[:, :, SEG], floor[:].to_broadcast([P, width // SEG]))
+            wide = bias_wide[c0 // HALF][:, c0 % HALF : c0 % HALF + width]
             nc.vector.tensor_tensor(
                 summed[:, :, 0:SEG],
                 bank[:].rearrange("p (j s) -> p j s", s=SEG),
-                bias_wide[h][:].rearrange("p (j s) -> p j s", s=SEG),
+                wide.rearrange("p (j s) -> p j s", s=SEG),
                 ADD,
             )
-            sums.append(summed)
-        for h in range(2):
-            nc.vector.tensor_reduce(best[:, h * runs : (h + 1) * runs], sums[h][:, :, 0 : SEG + 1], AXIS_X, MAX)
+            return summed
+
+        def take_maxima(k, summed):
+            c0, width = pieces[k]
+            nc.vector.tensor_reduce(best[:, c0 // SEG : (c0 + width) // SEG], summed[:, :, 0 : SEG + 1], AXIS_X, MAX)
+
+        sums = [add_biases(0), add_biases(1)]
+        take_maxima(0, sums[0])
+        sums.append(add_biases(2))
+        take_maxima(1, sums[1])
+        take_maxima(2, sums[2])
 
         nc.sync.dma_start(out[0], best[:])

@@ -44,29 +44,28 @@ def tile_attend_xtr_kernel(tc, qT, k_words, k_scales, kb, im, offs, out):
 
         offsets = keep.tile([P, N // 16], U16, name="offsets")
         nc.sync.dma_start(offsets[:], offs)
+        scales = shared.tile([P, T], U8, name="scales", align_bytes=64, offset=at_scales)
+        scale_words = scales[:].bitcast(I32)
+        nc.sync.dma_start(scale_words[P - 16 : P, :], k_scales[0].bitcast(I32))
         q_raw = shared.tile([P, PACK, NQ], F32, name="q_raw", align_bytes=64, offset=at_q_raw)
         nc.sync.dma_start(q_raw[:], qT[0].rearrange("(p j) w -> p j w", j=PACK))
         bias_row = shared.tile([P, T], F32, name="bias_row", align_bytes=64, offset=at_bias_row)
         nc.sync.dma_start(bias_row[KB_ROW:P, :], kb[0:1, :])
-
-        scales = shared.tile([P, T], U8, name="scales", align_bytes=64, offset=at_scales)
-        scale_words = scales[:].bitcast(I32)
-        nc.gpsimd.memset(scale_words[:, 512:1024], 0)
-        nc.vector.memset(scale_words[:, 0:255], 0)
-        nc.vector.memset(scale_words[:, 255:512], 0)
-        nc.sync.dma_start(scale_words[0:P:8, :], k_scales[0].bitcast(I32))
-        words = keep.tile([P, T], I32, name="words", align_bytes=64)
-        nc.sync.dma_start(words[:], k_words[0].rearrange("p n t -> p (n t)").bitcast(I32))
         floor = keep.tile([P, 1], F32, name="floor")
         nc.sync.dma_start(floor[:], im[0])
+        words = keep.tile([P, T], I32, name="words", align_bytes=64)
+        nc.sync.dma_start(words[:], k_words[0].rearrange("p n t -> p (n t)").bitcast(I32))
+
+        nc.vector.memset(scale_words[0 : P - 16, 0:511], 0)
+        nc.vector.memset(scale_words[0 : P - 16, 511:1024], 0)
 
         diagonal = keep.tile([P, P], F32, name="diagonal")
         nc.gpsimd.iota(diagonal[:], [[1, P]], base=0, channel_multiplier=-1, allow_small_or_imprecise_dtypes=True)
 
         bias_words = bias_row[0:KB_ROW, :].bitcast(I32)
-        nc.vector.memset(bias_words[:, 0:1023], 0)
-        nc.vector.memset(bias_words[:, 1023:2048], 0)
-        nc.gpsimd.memset(bias_words[:, 2048:T], 0)
+        nc.vector.memset(bias_words[:, 0:383], 0)
+        nc.vector.memset(bias_words[:, 383:768], 0)
+        nc.gpsimd.memset(bias_words[:, 768:T], 0)
 
         q_grouped = shared.tile([P, NQ * PACK], BF16, name="q_grouped", align_bytes=64, offset=at_q_grouped)
         nc.scalar.copy(q_grouped[:].rearrange("p (w j) -> p w j", j=PACK), q_raw[:].rearrange("p j w -> p w j"))
@@ -82,31 +81,36 @@ def tile_attend_xtr_kernel(tc, qT, k_words, k_scales, kb, im, offs, out):
         plane = shared.tile([P, N], U8, name="plane", align_bytes=64, offset=at_q_raw)
         nc.gpsimd.memset(plane[:].bitcast(I32), 0)
         for r in range(4):
-            nc.scalar.dma_start(plane[r:P:32, :].bitcast(I32), scales_listed[8 * r : P : 32, :].bitcast(I32))
+            nc.scalar.dma_start(plane[r:P:32, :].bitcast(I32), scales_listed[P - 16 + r : P : 4, :].bitcast(I32))
 
         q_codes = shared.tile([P, NQ], U32, name="q_codes", align_bytes=64, offset=at_bias_row + 8192)
         q_scales = keep.tile([P, NQ], U8, name="q_scales", align_bytes=64)
         nc.vector.quantize_mx(out=q_codes[:].bitcast(FP8X4), scales=q_scales[:], in_=q_grouped[:])
 
         cols = HALF // 16
+        piece = N // 4
         bias_cols = keep.tile([P, TILES], F32, name="bias_cols")
         bias_wide = []
         for h in range(2):
             bias_listed = shared.tile(
-                [P, HALF], F32, name="bias_listed%d" % h, align_bytes=64, offset=at_scales + 2560 * h
+                [P, HALF], F32, name="bias_listed%d" % h, align_bytes=64, offset=at_scales + 2048 * h
             )
             nc.vector.tensor_copy(bias_listed[:], bias_row[:].indirect(offsets[:, h * cols : (h + 1) * cols]))
-            turned = psum.tile([P, 4, P], F32, name="turned", tag="b%d" % h)
-            for i in range(4):
-                nc.tensor.transpose(turned[:, i, :], bias_listed[:, i * P : (i + 1) * P], ident[:])
-            nc.scalar.activation(bias_cols[:, 4 * h : 4 * h + 4], turned[:, :, KB_ROW], IDENTITY)
-            spread = psum.tile([P, 4, P], F32, name="spread", tag="b%d" % (2 + h))
-            for i in range(4):
-                t = 4 * h + i
-                nc.tensor.transpose(spread[:, i, :], bias_cols[:, t : t + 1].to_broadcast([P, P]), ident[:])
-            wide = keep.tile([P, HALF], F32, name="bias_wide%d" % h)
-            nc.scalar.copy(wide[:], spread[:].rearrange("p i n -> p (i n)"))
-            bias_wide.append(wide)
+            for u in range(2):
+                turned = psum.tile([P, 2, P], F32, name="turned", tag="turned%d" % u)
+                for i in range(2):
+                    c0 = (2 * u + i) * P
+                    nc.tensor.transpose(turned[:, i, :], bias_listed[:, c0 : c0 + P], ident[:])
+                t0 = 4 * h + 2 * u
+                nc.scalar.activation(bias_cols[:, t0 : t0 + 2], turned[:, :, KB_ROW], IDENTITY)
+            for u in range(2):
+                spread = psum.tile([P, 2, P], F32, name="spread", tag="spread%d" % u)
+                for i in range(2):
+                    t = 4 * h + 2 * u + i
+                    nc.tensor.transpose(spread[:, i, :], bias_cols[:, t : t + 1].to_broadcast([P, P]), ident[:])
+                wide = keep.tile([P, piece], F32, name="bias_wide%d" % (2 * h + u))
+                nc.scalar.copy(wide[:], spread[:].rearrange("p i n -> p (i n)"))
+                bias_wide.append(wide)
 
         words_listed = shared.tile([P, N], U32, name="words_listed", align_bytes=64, offset=at_q_grouped)
         for h in range(2):
@@ -116,39 +120,30 @@ def tile_attend_xtr_kernel(tc, qT, k_words, k_scales, kb, im, offs, out):
             )
 
         best = keep.tile([P, N // SEG], F32, name="best")
-        pieces = ((0, HALF), (HALF, HALF // 2), (HALF + HALF // 2, HALF // 2))
-
-        def add_biases(k):
-            c0, width = pieces[k]
-            bank = psum.tile([P, width], F32, name="bank", tag="s%d" % k)
-            nc.tensor.matmul_mx(
-                out=bank[:],
-                lhsT=q_codes[:].bitcast(FP8X4),
-                lhsT_scale=q_scales[:],
-                rhs=words_listed[:, c0 : c0 + width].bitcast(FP8X4),
-                rhs_scale=plane[:, c0 : c0 + width],
-                start=True,
-                stop=True,
-            )
-            summed = keep.tile([P, width // SEG, SEG + 4], F32, name="summed%d" % k)
-            nc.scalar.copy(summed[:, :, SEG], floor[:].to_broadcast([P, width // SEG]))
-            wide = bias_wide[c0 // HALF][:, c0 % HALF : c0 % HALF + width]
-            nc.vector.tensor_tensor(
-                summed[:, :, 0:SEG],
-                bank[:].rearrange("p (j s) -> p j s", s=SEG),
-                wide.rearrange("p (j s) -> p j s", s=SEG),
-                ADD,
-            )
-            return summed
-
-        def take_maxima(k, summed):
-            c0, width = pieces[k]
-            nc.vector.tensor_reduce(best[:, c0 // SEG : (c0 + width) // SEG], summed[:, :, 0 : SEG + 1], AXIS_X, MAX)
-
-        sums = [add_biases(0), add_biases(1)]
-        take_maxima(0, sums[0])
-        sums.append(add_biases(2))
-        take_maxima(1, sums[1])
-        take_maxima(2, sums[2])
+        runs = piece // SEG
+        for h in range(2):
+            sums = []
+            for k in (2 * h, 2 * h + 1):
+                bank = psum.tile([P, piece], F32, name="bank", tag="scores%d" % k)
+                nc.tensor.matmul_mx(
+                    out=bank[:],
+                    lhsT=q_codes[:].bitcast(FP8X4),
+                    lhsT_scale=q_scales[:],
+                    rhs=words_listed[:, k * piece : (k + 1) * piece].bitcast(FP8X4),
+                    rhs_scale=plane[:, k * piece : (k + 1) * piece],
+                    start=True,
+                    stop=True,
+                )
+                summed = keep.tile([P, runs, SEG + 4], F32, name="summed%d" % k)
+                nc.scalar.copy(summed[:, :, SEG], floor[:].to_broadcast([P, runs]))
+                nc.vector.tensor_tensor(
+                    summed[:, :, 0:SEG],
+                    bank[:].rearrange("p (j s) -> p j s", s=SEG),
+                    bias_wide[k][:].rearrange("p (j s) -> p j s", s=SEG),
+                    ADD,
+                )
+                sums.append((k, summed))
+            for k, summed in sums:
+                nc.vector.tensor_reduce(best[:, k * runs : (k + 1) * runs], summed[:, :, 0 : SEG + 1], AXIS_X, MAX)
 
         nc.sync.dma_start(out[0], best[:])

@@ -96,21 +96,17 @@ def tile_attend_xtr_kernel(tc, qT, k_words, k_scales, kb, im, offs, out):
                 [P, HALF], F32, name="bias_listed%d" % h, align_bytes=64, offset=at_scales + 2048 * h
             )
             nc.vector.tensor_copy(bias_listed[:], bias_row[:].indirect(offsets[:, h * cols : (h + 1) * cols]))
-            for u in range(2):
-                turned = psum.tile([P, 2, P], F32, name="turned", tag="turned%d" % u)
-                for i in range(2):
-                    c0 = (2 * u + i) * P
-                    nc.tensor.transpose(turned[:, i, :], bias_listed[:, c0 : c0 + P], ident[:])
-                t0 = 4 * h + 2 * u
-                nc.scalar.activation(bias_cols[:, t0 : t0 + 2], turned[:, :, KB_ROW], IDENTITY)
-            for u in range(2):
-                spread = psum.tile([P, 2, P], F32, name="spread", tag="spread%d" % u)
-                for i in range(2):
-                    t = 4 * h + 2 * u + i
-                    nc.tensor.transpose(spread[:, i, :], bias_cols[:, t : t + 1].to_broadcast([P, P]), ident[:])
-                wide = keep.tile([P, piece], F32, name="bias_wide%d" % (2 * h + u))
-                nc.scalar.copy(wide[:], spread[:].rearrange("p i n -> p (i n)"))
-                bias_wide.append(wide)
+            turned = psum.tile([P, 4, P], F32, name="turned", tag="b%d" % h)
+            for i in range(4):
+                nc.tensor.transpose(turned[:, i, :], bias_listed[:, i * P : (i + 1) * P], ident[:])
+            nc.scalar.activation(bias_cols[:, 4 * h : 4 * h + 4], turned[:, :, KB_ROW], IDENTITY)
+            spread = psum.tile([P, 4, P], F32, name="spread", tag="b%d" % (2 + h))
+            for i in range(4):
+                t = 4 * h + i
+                nc.tensor.transpose(spread[:, i, :], bias_cols[:, t : t + 1].to_broadcast([P, P]), ident[:])
+            wide = keep.tile([P, HALF], F32, name="bias_wide%d" % h)
+            nc.scalar.copy(wide[:], spread[:].rearrange("p i n -> p (i n)"))
+            bias_wide.append(wide)
 
         words_listed = shared.tile([P, N], U32, name="words_listed", align_bytes=64, offset=at_q_grouped)
         for h in range(2):
@@ -121,9 +117,14 @@ def tile_attend_xtr_kernel(tc, qT, k_words, k_scales, kb, im, offs, out):
 
         best = keep.tile([P, N // SEG], F32, name="best")
         runs = piece // SEG
+        sums = []
+        for u in range(2):
+            summed = keep.tile([P, runs, SEG + 4], F32, name="summed%d" % u)
+            nc.scalar.copy(summed[:, :, SEG], floor[:].to_broadcast([P, runs]))
+            sums.append(summed)
         for h in range(2):
-            sums = []
-            for k in (2 * h, 2 * h + 1):
+            for u in range(2):
+                k = 2 * h + u
                 bank = psum.tile([P, piece], F32, name="bank", tag="scores%d" % k)
                 nc.tensor.matmul_mx(
                     out=bank[:],
@@ -134,16 +135,14 @@ def tile_attend_xtr_kernel(tc, qT, k_words, k_scales, kb, im, offs, out):
                     start=True,
                     stop=True,
                 )
-                summed = keep.tile([P, runs, SEG + 4], F32, name="summed%d" % k)
-                nc.scalar.copy(summed[:, :, SEG], floor[:].to_broadcast([P, runs]))
                 nc.vector.tensor_tensor(
-                    summed[:, :, 0:SEG],
+                    sums[u][:, :, 0:SEG],
                     bank[:].rearrange("p (j s) -> p j s", s=SEG),
-                    bias_wide[k][:].rearrange("p (j s) -> p j s", s=SEG),
+                    bias_wide[h][:, u * piece : (u + 1) * piece].rearrange("p (j s) -> p j s", s=SEG),
                     ADD,
                 )
-                sums.append((k, summed))
-            for k, summed in sums:
-                nc.vector.tensor_reduce(best[:, k * runs : (k + 1) * runs], summed[:, :, 0 : SEG + 1], AXIS_X, MAX)
+            for u in range(2):
+                k = 2 * h + u
+                nc.vector.tensor_reduce(best[:, k * runs : (k + 1) * runs], sums[u][:, :, 0 : SEG + 1], AXIS_X, MAX)
 
         nc.sync.dma_start(out[0], best[:])

@@ -54,7 +54,9 @@ def tile_attend_xtr_kernel(tc, qT, k_words, k_scales, kb, im, offs, out):
         floor = keep.tile([P, 1], F32, name="floor")
         nc.sync.dma_start(floor[:], im[0])
         words = keep.tile([P, T], I32, name="words", align_bytes=64)
-        nc.sync.dma_start(words[:], k_words[0].rearrange("p n t -> p (n t)").bitcast(I32))
+        words_hbm = k_words[0].rearrange("p n t -> p (n t)").bitcast(I32)
+        for c0 in range(0, T, 1024):
+            nc.sync.dma_start(words[:, c0 : c0 + 1024], words_hbm[:, c0 : c0 + 1024])
 
         nc.vector.memset(scale_words[0 : P - 16, 0:511], 0)
         nc.vector.memset(scale_words[0 : P - 16, 511:1024], 0)

@@ -90,7 +90,6 @@ def tile_attend_xtr_kernel(tc, qT, k_words, k_scales, kb, im, offs, out):
         nc.vector.quantize_mx(out=q_codes[:].bitcast(FP8X4), scales=q_scales[:], in_=q_grouped[:])
 
         cols = HALF // 16
-        piece = N // 4
         bias_cols = keep.tile([P, TILES], F32, name="bias_cols")
         bias_wide = []
         for h in range(2):
@@ -107,7 +106,8 @@ def tile_attend_xtr_kernel(tc, qT, k_words, k_scales, kb, im, offs, out):
                 t = 4 * h + i
                 nc.tensor.transpose(spread[:, i, :], bias_cols[:, t : t + 1].to_broadcast([P, P]), ident[:])
             wide = keep.tile([P, HALF], F32, name="bias_wide%d" % h)
-            nc.scalar.copy(wide[:], spread[:].rearrange("p i n -> p (i n)"))
+            for c0, c1 in ((0, HALF),) if h == 0 else ((0, HALF // 2), (HALF // 2, HALF)):
+                nc.scalar.copy(wide[:, c0:c1], spread[:].rearrange("p i n -> p (i n)")[:, c0:c1])
             bias_wide.append(wide)
 
         words_listed = shared.tile([P, N], U32, name="words_listed", align_bytes=64, offset=at_q_grouped)
@@ -117,34 +117,32 @@ def tile_attend_xtr_kernel(tc, qT, k_words, k_scales, kb, im, offs, out):
                 words[:].bitcast(U32).indirect(offsets[:, h * cols : (h + 1) * cols]),
             )
 
-        best = keep.tile([P, N // SEG], F32, name="best")
-        runs = piece // SEG
+        runs = HALF // SEG
         sums = []
-        for u in range(2):
-            summed = keep.tile([P, runs, SEG + 4], F32, name="summed%d" % u)
+        for h in range(2):
+            summed = keep.tile([P, runs, SEG + 4], F32, name="summed%d" % h)
             nc.scalar.copy(summed[:, :, SEG], floor[:].to_broadcast([P, runs]))
             sums.append(summed)
+        for c0, width in ((0, HALF), (HALF, HALF // 2), (HALF + HALF // 2, HALF // 2)):
+            bank = psum.tile([P, width], F32, name="bank", tag="scores%d" % c0)
+            nc.tensor.matmul_mx(
+                out=bank[:],
+                lhsT=q_codes[:].bitcast(FP8X4),
+                lhsT_scale=q_scales[:],
+                rhs=words_listed[:, c0 : c0 + width].bitcast(FP8X4),
+                rhs_scale=plane[:, c0 : c0 + width],
+                start=True,
+                stop=True,
+            )
+            h, first = divmod(c0, HALF)
+            nc.vector.tensor_tensor(
+                sums[h][:, first // SEG : (first + width) // SEG, 0:SEG],
+                bank[:].rearrange("p (j s) -> p j s", s=SEG),
+                bias_wide[h][:, first : first + width].rearrange("p (j s) -> p j s", s=SEG),
+                ADD,
+            )
+        best = keep.tile([P, N // SEG], F32, name="best")
         for h in range(2):
-            for u in range(2):
-                k = 2 * h + u
-                bank = psum.tile([P, piece], F32, name="bank", tag="scores%d" % k)
-                nc.tensor.matmul_mx(
-                    out=bank[:],
-                    lhsT=q_codes[:].bitcast(FP8X4),
-                    lhsT_scale=q_scales[:],
-                    rhs=words_listed[:, k * piece : (k + 1) * piece].bitcast(FP8X4),
-                    rhs_scale=plane[:, k * piece : (k + 1) * piece],
-                    start=True,
-                    stop=True,
-                )
-                nc.vector.tensor_tensor(
-                    sums[u][:, :, 0:SEG],
-                    bank[:].rearrange("p (j s) -> p j s", s=SEG),
-                    bias_wide[h][:, u * piece : (u + 1) * piece].rearrange("p (j s) -> p j s", s=SEG),
-                    ADD,
-                )
-            for u in range(2):
-                k = 2 * h + u
-                nc.vector.tensor_reduce(best[:, k * runs : (k + 1) * runs], sums[u][:, :, 0 : SEG + 1], AXIS_X, MAX)
+            nc.vector.tensor_reduce(best[:, h * runs : (h + 1) * runs], sums[h][:, :, 0 : SEG + 1], AXIS_X, MAX)
 
         nc.sync.dma_start(out[0], best[:])

@@ -46,28 +46,29 @@ def tile_attend_xtr_kernel(tc, qT, k_words, k_scales, kb, im, offs, out):
         nc.sync.dma_start(offsets[:], offs)
         scales = shared.tile([P, T], U8, name="scales", align_bytes=64, offset=at_scales)
         scale_words = scales[:].bitcast(I32)
-        nc.sync.dma_start(scale_words[P - 16 : P, :], k_scales[0].bitcast(I32))
+        nc.sync.dma_start(scale_words[48:64, :], k_scales[0].bitcast(I32))
         q_raw = shared.tile([P, PACK, NQ], F32, name="q_raw", align_bytes=64, offset=at_q_raw)
         nc.sync.dma_start(q_raw[:], qT[0].rearrange("(p j) w -> p j w", j=PACK))
         bias_row = shared.tile([P, T], F32, name="bias_row", align_bytes=64, offset=at_bias_row)
         nc.sync.dma_start(bias_row[KB_ROW:P, :], kb[0:1, :])
-        floor = keep.tile([P, 1], F32, name="floor")
-        nc.sync.dma_start(floor[:], im[0])
         words = keep.tile([P, T], I32, name="words", align_bytes=64)
         words_hbm = k_words[0].rearrange("p n t -> p (n t)").bitcast(I32)
         for c0 in range(0, T, 1024):
             nc.sync.dma_start(words[:, c0 : c0 + 1024], words_hbm[:, c0 : c0 + 1024])
+        floor = keep.tile([P, 1], F32, name="floor")
+        nc.sync.dma_start(floor[:], im[0])
 
-        nc.vector.memset(scale_words[0 : P - 16, 0:511], 0)
-        nc.vector.memset(scale_words[0 : P - 16, 511:1024], 0)
+        nc.vector.memset(scale_words[0:48, 0:511], 0)
+        nc.vector.memset(scale_words[0:48, 511:1024], 0)
+        nc.gpsimd.memset(scale_words[64:P, :], 0)
 
         diagonal = keep.tile([P, P], F32, name="diagonal")
         nc.gpsimd.iota(diagonal[:], [[1, P]], base=0, channel_multiplier=-1, allow_small_or_imprecise_dtypes=True)
 
         bias_words = bias_row[0:KB_ROW, :].bitcast(I32)
-        nc.vector.memset(bias_words[:, 0:383], 0)
-        nc.vector.memset(bias_words[:, 383:768], 0)
-        nc.gpsimd.memset(bias_words[:, 768:T], 0)
+        nc.vector.memset(bias_words[:, 0:575], 0)
+        nc.vector.memset(bias_words[:, 575:1152], 0)
+        nc.gpsimd.memset(bias_words[:, 1152:T], 0)
 
         q_grouped = shared.tile([P, NQ * PACK], BF16, name="q_grouped", align_bytes=64, offset=at_q_grouped)
         nc.scalar.copy(q_grouped[:].rearrange("p (w j) -> p w j", j=PACK), q_raw[:].rearrange("p j w -> p w j"))
@@ -83,7 +84,8 @@ def tile_attend_xtr_kernel(tc, qT, k_words, k_scales, kb, im, offs, out):
         plane = shared.tile([P, N], U8, name="plane", align_bytes=64, offset=at_q_raw)
         nc.gpsimd.memset(plane[:].bitcast(I32), 0)
         for r in range(4):
-            nc.scalar.dma_start(plane[r:P:32, :].bitcast(I32), scales_listed[P - 16 + r : P : 4, :].bitcast(I32))
+            queue = nc.scalar if r % 2 else nc.sync
+            queue.dma_start(plane[r:P:32, :].bitcast(I32), scales_listed[48 + r : 64 : 4, :].bitcast(I32))
 
         q_codes = shared.tile([P, NQ], U32, name="q_codes", align_bytes=64, offset=at_bias_row + 8192)
         q_scales = keep.tile([P, NQ], U8, name="q_scales", align_bytes=64)
@@ -123,7 +125,7 @@ def tile_attend_xtr_kernel(tc, qT, k_words, k_scales, kb, im, offs, out):
             summed = keep.tile([P, runs, SEG + 4], F32, name="summed%d" % h)
             nc.scalar.copy(summed[:, :, SEG], floor[:].to_broadcast([P, runs]))
             sums.append(summed)
-        for c0, width in ((0, HALF), (HALF, HALF // 2), (HALF + HALF // 2, HALF // 2)):
+        for c0, width in [(c0, HALF // 2) for c0 in range(0, N, HALF // 2)]:
             bank = psum.tile([P, width], F32, name="bank", tag="scores%d" % c0)
             nc.tensor.matmul_mx(
                 out=bank[:],

@@ -66,9 +66,9 @@ def tile_attend_xtr_kernel(tc, qT, k_words, k_scales, kb, im, offs, out):
         nc.gpsimd.iota(diagonal[:], [[1, P]], base=0, channel_multiplier=-1, allow_small_or_imprecise_dtypes=True)
 
         bias_words = bias_row[0:KB_ROW, :].bitcast(I32)
-        nc.vector.memset(bias_words[:, 0:575], 0)
-        nc.vector.memset(bias_words[:, 575:1152], 0)
-        nc.gpsimd.memset(bias_words[:, 1152:T], 0)
+        nc.vector.memset(bias_words[:, 0:687], 0)
+        nc.vector.memset(bias_words[:, 687:1376], 0)
+        nc.gpsimd.memset(bias_words[:, 1376:T], 0)
 
         q_grouped = shared.tile([P, NQ * PACK], BF16, name="q_grouped", align_bytes=64, offset=at_q_grouped)
         nc.scalar.copy(q_grouped[:].rearrange("p (w j) -> p w j", j=PACK), q_raw[:].rearrange("p j w -> p w j"))

@@ -42,6 +42,8 @@ def tile_attend_xtr_kernel(tc, qT, k_words, k_scales, kb, im, offs, out):
         at_bias_row = 6 * 1024
         at_q_raw = at_bias_row + 4 * T
 
+        bias_row = shared.tile([P, T], F32, name="bias_row", align_bytes=64, offset=at_bias_row)
+        nc.sync.dma_start(bias_row[KB_ROW:P, :], kb[0:1, :])
         offsets = keep.tile([P, N // 16], U16, name="offsets")
         nc.sync.dma_start(offsets[:], offs)
         scales = shared.tile([P, T], U8, name="scales", align_bytes=64, offset=at_scales)
@@ -49,12 +51,10 @@ def tile_attend_xtr_kernel(tc, qT, k_words, k_scales, kb, im, offs, out):
         nc.sync.dma_start(scale_words[48:64, :], k_scales[0].bitcast(I32))
         q_raw = shared.tile([P, PACK, NQ], F32, name="q_raw", align_bytes=64, offset=at_q_raw)
         nc.sync.dma_start(q_raw[:], qT[0].rearrange("(p j) w -> p j w", j=PACK))
-        bias_row = shared.tile([P, T], F32, name="bias_row", align_bytes=64, offset=at_bias_row)
-        nc.sync.dma_start(bias_row[KB_ROW:P, :], kb[0:1, :])
         words = keep.tile([P, T], I32, name="words", align_bytes=64)
         words_hbm = k_words[0].rearrange("p n t -> p (n t)").bitcast(I32)
-        for c0 in range(0, T, 1024):
-            nc.sync.dma_start(words[:, c0 : c0 + 1024], words_hbm[:, c0 : c0 + 1024])
+        for c0 in range(0, T, 2048):
+            nc.sync.dma_start(words[:, c0 : c0 + 2048], words_hbm[:, c0 : c0 + 2048])
         floor = keep.tile([P, 1], F32, name="floor")
         nc.sync.dma_start(floor[:], im[0])
 

@@ -9,7 +9,7 @@ U32 = mybir.dt.uint32
 U16 = mybir.dt.uint16
 U8 = mybir.dt.uint8
 FP8X4 = mybir.dt.float8_e4m3fn_x4
-IDENTITY = mybir.ActivationFunctionType.Identity
+COPY = mybir.ActivationFunctionType.Copy
 ABS = mybir.ActivationFunctionType.Abs
 RELU = mybir.ActivationFunctionType.Relu
 MAX = mybir.AluOpType.max
@@ -23,6 +23,7 @@ N = 1024
 NQ = 128
 SEG = 32
 HALF = N // 2
+QUARTER = N // 4
 TILES = N // P
 KB_ROW = P - 1
 
@@ -37,96 +38,98 @@ def tile_attend_xtr_kernel(tc, qT, k_words, k_scales, kb, im, offs, out):
         shared = ctx.enter_context(tc.tile_pool(name="shared", bufs=1))
         psum = ctx.enter_context(tc.psum_pool(name="psum", bufs=1))
 
-        at_scales = 0
-        at_q_grouped = 5 * 1024
-        at_bias_row = 6 * 1024
-        at_q_raw = at_bias_row + 4 * T
+        at_words = 0
+        at_scales = 4 * T
+        at_sums = 5 * T
 
-        bias_row = shared.tile([P, T], F32, name="bias_row", align_bytes=64, offset=at_bias_row)
+        bias_row = keep.tile([P, T], F32, name="bias_row", align_bytes=64)
         nc.sync.dma_start(bias_row[KB_ROW:P, :], kb[0:1, :])
         offsets = keep.tile([P, N // 16], U16, name="offsets")
         nc.sync.dma_start(offsets[:], offs)
-        scales = shared.tile([P, T], U8, name="scales", align_bytes=64, offset=at_scales)
-        scale_words = scales[:].bitcast(I32)
-        nc.sync.dma_start(scale_words[48:64, :], k_scales[0].bitcast(I32))
-        q_raw = shared.tile([P, PACK, NQ], F32, name="q_raw", align_bytes=64, offset=at_q_raw)
+        q_raw = keep.tile([P, PACK, NQ], F32, name="q_raw", align_bytes=64)
         nc.sync.dma_start(q_raw[:], qT[0].rearrange("(p j) w -> p j w", j=PACK))
-        words = keep.tile([P, T], I32, name="words", align_bytes=64)
-        words_hbm = k_words[0].rearrange("p n t -> p (n t)").bitcast(I32)
-        for c0 in range(0, T, 2048):
-            nc.sync.dma_start(words[:, c0 : c0 + 2048], words_hbm[:, c0 : c0 + 2048])
-        floor = keep.tile([P, 1], F32, name="floor")
-        nc.sync.dma_start(floor[:], im[0])
-
-        nc.vector.memset(scale_words[0:48, 0:511], 0)
-        nc.vector.memset(scale_words[0:48, 511:1024], 0)
-        nc.gpsimd.memset(scale_words[64:P, :], 0)
 
         diagonal = keep.tile([P, P], F32, name="diagonal")
         nc.gpsimd.iota(diagonal[:], [[1, P]], base=0, channel_multiplier=-1, allow_small_or_imprecise_dtypes=True)
 
+        scales = shared.tile([P, T], U8, name="scales", align_bytes=64, offset=at_scales)
+        scale_words = scales[:].bitcast(I32)
+        nc.vector.memset(scale_words, 0)
+        nc.sync.dma_start(scale_words[32:96:4, :], k_scales[0].bitcast(I32))
+
         bias_words = bias_row[0:KB_ROW, :].bitcast(I32)
-        nc.vector.memset(bias_words[:, 0:687], 0)
-        nc.vector.memset(bias_words[:, 687:1376], 0)
-        nc.gpsimd.memset(bias_words[:, 1376:T], 0)
+        nc.vector.memset(bias_words[:, 0:1055], 0)
+        nc.vector.memset(bias_words[:, 1055:2112], 0)
+        nc.gpsimd.memset(bias_words[:, 2112:T], 0)
 
-        q_grouped = shared.tile([P, NQ * PACK], BF16, name="q_grouped", align_bytes=64, offset=at_q_grouped)
-        nc.scalar.copy(q_grouped[:].rearrange("p (w j) -> p w j", j=PACK), q_raw[:].rearrange("p j w -> p w j"))
-
-        ident = keep.tile([P, P], F32, name="ident")
         distance = keep.tile([P, P], F32, name="distance")
         nc.scalar.activation(distance[:], diagonal[:], ABS)
+        ident = keep.tile([P, P], F32, name="ident")
         nc.scalar.activation(ident[:], distance[:], RELU, bias=1.0, scale=-1.0)
+
+        words = shared.tile([P, T], I32, name="words", align_bytes=64, offset=at_words)
+        words_hbm = k_words[0].rearrange("p n t -> p (n t)").bitcast(I32)
+        for c0 in range(0, T, 2048):
+            nc.sync.dma_start(words[:, c0 : c0 + 2048], words_hbm[:, c0 : c0 + 2048])
+
+        plane = keep.tile([P, N], U8, name="plane", align_bytes=64)
+        nc.gpsimd.memset(plane[:].bitcast(I32), 0)
+
+        q_grouped = keep.tile([P, NQ * PACK], BF16, name="q_grouped", align_bytes=64)
+        nc.scalar.activation(
+            q_grouped[:].rearrange("p (w j) -> p w j", j=PACK), q_raw[:].rearrange("p j w -> p w j"), COPY
+        )
 
         scales_listed = keep.tile([P, N], U8, name="scales_listed", align_bytes=64)
         nc.vector.tensor_copy(scales_listed[:], scales[:].indirect(offsets[:]))
-
-        plane = shared.tile([P, N], U8, name="plane", align_bytes=64, offset=at_q_raw)
-        nc.gpsimd.memset(plane[:].bitcast(I32), 0)
         for r in range(4):
-            queue = nc.scalar if r % 2 else nc.sync
-            queue.dma_start(plane[r:P:32, :].bitcast(I32), scales_listed[48 + r : 64 : 4, :].bitcast(I32))
+            nc.sync.dma_start(plane[r:P:32, :].bitcast(I32), scales_listed[32 + 4 * r : 96 : 16, :].bitcast(I32))
+        floor = shared.tile([P, 1], F32, name="floor", align_bytes=64, offset=at_scales)
+        nc.sync.dma_start(floor[:], im[0])
 
-        q_codes = shared.tile([P, NQ], U32, name="q_codes", align_bytes=64, offset=at_bias_row + 8192)
+        q_codes = keep.tile([P, NQ], U32, name="q_codes", align_bytes=64)
         q_scales = keep.tile([P, NQ], U8, name="q_scales", align_bytes=64)
         nc.vector.quantize_mx(out=q_codes[:].bitcast(FP8X4), scales=q_scales[:], in_=q_grouped[:])
 
-        cols = HALF // 16
-        bias_cols = keep.tile([P, TILES], F32, name="bias_cols")
-        bias_wide = []
-        for h in range(2):
-            bias_listed = shared.tile(
-                [P, HALF], F32, name="bias_listed%d" % h, align_bytes=64, offset=at_scales + 2048 * h
+        cols = QUARTER // 16
+        bias_listed = keep.tile([P, N], F32, name="bias_listed", align_bytes=64)
+        for g in range(4):
+            nc.scalar.activation(
+                bias_listed[:, g * QUARTER : (g + 1) * QUARTER],
+                bias_row[:].indirect(offsets[:, g * cols : (g + 1) * cols]),
+                COPY,
             )
-            nc.vector.tensor_copy(bias_listed[:], bias_row[:].indirect(offsets[:, h * cols : (h + 1) * cols]))
+        bias_cols = shared.tile([P, TILES], F32, name="bias_cols", align_bytes=64, offset=at_sums)
+        for h in range(2):
             turned = psum.tile([P, 4, P], F32, name="turned", tag="b%d" % h)
             for i in range(4):
-                nc.tensor.transpose(turned[:, i, :], bias_listed[:, i * P : (i + 1) * P], ident[:])
-            nc.scalar.activation(bias_cols[:, 4 * h : 4 * h + 4], turned[:, :, KB_ROW], IDENTITY)
+                t = 4 * h + i
+                nc.tensor.transpose(turned[:, i, :], bias_listed[:, t * P : (t + 1) * P], ident[:])
+            nc.scalar.copy(bias_cols[:, 4 * h : 4 * h + 4], turned[:, :, KB_ROW])
+        bias_wide = keep.tile([P, N], F32, name="bias_wide")
+        for h in range(2):
             spread = psum.tile([P, 4, P], F32, name="spread", tag="b%d" % (2 + h))
             for i in range(4):
                 t = 4 * h + i
                 nc.tensor.transpose(spread[:, i, :], bias_cols[:, t : t + 1].to_broadcast([P, P]), ident[:])
-            wide = keep.tile([P, HALF], F32, name="bias_wide%d" % h)
-            for c0, c1 in ((0, HALF),) if h == 0 else ((0, HALF // 2), (HALF // 2, HALF)):
-                nc.scalar.copy(wide[:, c0:c1], spread[:].rearrange("p i n -> p (i n)")[:, c0:c1])
-            bias_wide.append(wide)
+            for c0, c1 in ((0, HALF),) if h == 0 else ((0, QUARTER), (QUARTER, HALF)):
+                nc.scalar.copy(
+                    bias_wide[:, h * HALF + c0 : h * HALF + c1], spread[:].rearrange("p i n -> p (i n)")[:, c0:c1]
+                )
 
-        words_listed = shared.tile([P, N], U32, name="words_listed", align_bytes=64, offset=at_q_grouped)
-        for h in range(2):
+        summed = shared.tile([P, N // SEG, SEG + 4], F32, name="summed", align_bytes=64, offset=at_sums)
+        nc.scalar.copy(summed[:, :, SEG], floor[:].to_broadcast([P, N // SEG]))
+
+        words_listed = keep.tile([P, N], U32, name="words_listed", align_bytes=64)
+        for g in range(4):
             nc.vector.tensor_copy(
-                words_listed[:, h * HALF : (h + 1) * HALF],
-                words[:].bitcast(U32).indirect(offsets[:, h * cols : (h + 1) * cols]),
+                words_listed[:, g * QUARTER : (g + 1) * QUARTER],
+                words[:].bitcast(U32).indirect(offsets[:, g * cols : (g + 1) * cols]),
             )
 
-        runs = HALF // SEG
-        sums = []
-        for h in range(2):
-            summed = keep.tile([P, runs, SEG + 4], F32, name="summed%d" % h)
-            nc.scalar.copy(summed[:, :, SEG], floor[:].to_broadcast([P, runs]))
-            sums.append(summed)
-        for c0, width in [(c0, HALF // 2) for c0 in range(0, N, HALF // 2)]:
-            bank = psum.tile([P, width], F32, name="bank", tag="scores%d" % c0)
+        c0 = 0
+        for width, tag in ((P, "b0"), (P, "b4"), (QUARTER, "b5"), (QUARTER, "b6"), (QUARTER, "b7")):
+            bank = psum.tile([P, width], F32, name="bank", tag=tag)
             nc.tensor.matmul_mx(
                 out=bank[:],
                 lhsT=q_codes[:].bitcast(FP8X4),
@@ -136,15 +139,18 @@ def tile_attend_xtr_kernel(tc, qT, k_words, k_scales, kb, im, offs, out):
                 start=True,
                 stop=True,
             )
-            h, first = divmod(c0, HALF)
             nc.vector.tensor_tensor(
-                sums[h][:, first // SEG : (first + width) // SEG, 0:SEG],
+                summed[:, c0 // SEG : (c0 + width) // SEG, 0:SEG],
                 bank[:].rearrange("p (j s) -> p j s", s=SEG),
-                bias_wide[h][:, first : first + width].rearrange("p (j s) -> p j s", s=SEG),
+                bias_wide[:, c0 : c0 + width].rearrange("p (j s) -> p j s", s=SEG),
                 ADD,
             )
+            c0 = c0 + width
         best = keep.tile([P, N // SEG], F32, name="best")
+        runs = HALF // SEG
         for h in range(2):
-            nc.vector.tensor_reduce(best[:, h * runs : (h + 1) * runs], sums[h][:, :, 0 : SEG + 1], AXIS_X, MAX)
+            nc.vector.tensor_reduce(
+                best[:, h * runs : (h + 1) * runs], summed[:, h * runs : (h + 1) * runs, 0 : SEG + 1], AXIS_X, MAX
+            )
 
         nc.sync.dma_start(out[0], best[:])

@@ -82,23 +82,26 @@ def tile_attend_xtr_kernel(tc, qT, k_words, k_scales, kb, im, offs, out):
 
         scales_listed = keep.tile([P, N], U8, name="scales_listed", align_bytes=64)
         nc.vector.tensor_copy(scales_listed[:], scales[:].indirect(offsets[:]))
-        for r in range(4):
-            nc.sync.dma_start(plane[r:P:32, :].bitcast(I32), scales_listed[32 + 4 * r : 96 : 16, :].bitcast(I32))
-        floor = shared.tile([P, 1], F32, name="floor", align_bytes=64, offset=at_scales)
-        nc.sync.dma_start(floor[:], im[0])
-
-        q_codes = keep.tile([P, NQ], U32, name="q_codes", align_bytes=64)
-        q_scales = keep.tile([P, NQ], U8, name="q_scales", align_bytes=64)
-        nc.vector.quantize_mx(out=q_codes[:].bitcast(FP8X4), scales=q_scales[:], in_=q_grouped[:])
-
         cols = QUARTER // 16
         bias_listed = keep.tile([P, N], F32, name="bias_listed", align_bytes=64)
-        for g in range(4):
+        for g in range(2):
             nc.scalar.activation(
                 bias_listed[:, g * QUARTER : (g + 1) * QUARTER],
                 bias_row[:].indirect(offsets[:, g * cols : (g + 1) * cols]),
                 COPY,
             )
+        for r in range(4):
+            queue = nc.scalar if r % 2 else nc.sync
+            queue.dma_start(plane[r:P:32, :].bitcast(I32), scales_listed[32 + 4 * r : 96 : 16, :].bitcast(I32))
+        floor = shared.tile([P, 1], F32, name="floor", align_bytes=64, offset=at_scales)
+        nc.sync.dma_start(floor[:], im[0])
+
+        nc.vector.tensor_copy(bias_listed[:, HALF:N], bias_row[:].indirect(offsets[:, 2 * cols : 4 * cols]))
+
+        q_codes = keep.tile([P, NQ], U32, name="q_codes", align_bytes=64)
+        q_scales = keep.tile([P, NQ], U8, name="q_scales", align_bytes=64)
+        nc.vector.quantize_mx(out=q_codes[:].bitcast(FP8X4), scales=q_scales[:], in_=q_grouped[:])
+
         bias_cols = shared.tile([P, TILES], F32, name="bias_cols", align_bytes=64, offset=at_sums)
         for h in range(2):
             turned = psum.tile([P, 4, P], F32, name="turned", tag="b%d" % h)

@@ -38,39 +38,41 @@ def tile_attend_xtr_kernel(tc, qT, k_words, k_scales, kb, im, offs, out):
         shared = ctx.enter_context(tc.tile_pool(name="shared", bufs=1))
         psum = ctx.enter_context(tc.psum_pool(name="psum", bufs=1))
 
-        at_words = 0
-        at_scales = 4 * T
-        at_sums = 5 * T
+        at_sums = 0
 
         bias_row = keep.tile([P, T], F32, name="bias_row", align_bytes=64)
         nc.sync.dma_start(bias_row[KB_ROW:P, :], kb[0:1, :])
         offsets = keep.tile([P, N // 16], U16, name="offsets")
         nc.sync.dma_start(offsets[:], offs)
+        scales = keep.tile([P, T], U8, name="scales", align_bytes=64)
+        scale_words = scales[:].bitcast(I32)
+        nc.sync.dma_start(scale_words[48:64, :], k_scales[0].bitcast(I32))
         q_raw = keep.tile([P, PACK, NQ], F32, name="q_raw", align_bytes=64)
         nc.sync.dma_start(q_raw[:], qT[0].rearrange("(p j) w -> p j w", j=PACK))
+
+        nc.vector.memset(scale_words[0:48, 0:511], 0)
+        nc.vector.memset(scale_words[0:48, 511:1024], 0)
+        nc.gpsimd.memset(scale_words[64:P, :], 0)
 
         diagonal = keep.tile([P, P], F32, name="diagonal")
         nc.gpsimd.iota(diagonal[:], [[1, P]], base=0, channel_multiplier=-1, allow_small_or_imprecise_dtypes=True)
 
-        scales = shared.tile([P, T], U8, name="scales", align_bytes=64, offset=at_scales)
-        scale_words = scales[:].bitcast(I32)
-        nc.vector.memset(scale_words, 0)
-        nc.sync.dma_start(scale_words[32:96:4, :], k_scales[0].bitcast(I32))
-
         bias_words = bias_row[0:KB_ROW, :].bitcast(I32)
-        nc.vector.memset(bias_words[:, 0:1055], 0)
-        nc.vector.memset(bias_words[:, 1055:2112], 0)
-        nc.gpsimd.memset(bias_words[:, 2112:T], 0)
+        nc.vector.memset(bias_words[:, 0:991], 0)
+        nc.vector.memset(bias_words[:, 991:1984], 0)
+        nc.gpsimd.memset(bias_words[:, 1984:T], 0)
 
         distance = keep.tile([P, P], F32, name="distance")
         nc.scalar.activation(distance[:], diagonal[:], ABS)
         ident = keep.tile([P, P], F32, name="ident")
         nc.scalar.activation(ident[:], distance[:], RELU, bias=1.0, scale=-1.0)
 
-        words = shared.tile([P, T], I32, name="words", align_bytes=64, offset=at_words)
+        words = keep.tile([P, T], I32, name="words", align_bytes=64)
         words_hbm = k_words[0].rearrange("p n t -> p (n t)").bitcast(I32)
         for c0 in range(0, T, 2048):
             nc.sync.dma_start(words[:, c0 : c0 + 2048], words_hbm[:, c0 : c0 + 2048])
+        floor = keep.tile([P, 1], F32, name="floor")
+        nc.sync.dma_start(floor[:], im[0])
 
         plane = keep.tile([P, N], U8, name="plane", align_bytes=64)
         nc.gpsimd.memset(plane[:].bitcast(I32), 0)
@@ -92,9 +94,7 @@ def tile_attend_xtr_kernel(tc, qT, k_words, k_scales, kb, im, offs, out):
             )
         for r in range(4):
             queue = nc.scalar if r % 2 else nc.sync
-            queue.dma_start(plane[r:P:32, :].bitcast(I32), scales_listed[32 + 4 * r : 96 : 16, :].bitcast(I32))
-        floor = shared.tile([P, 1], F32, name="floor", align_bytes=64, offset=at_scales)
-        nc.sync.dma_start(floor[:], im[0])
+            queue.dma_start(plane[r:P:32, :].bitcast(I32), scales_listed[48 + r : 64 : 4, :].bitcast(I32))
 
         nc.vector.tensor_copy(bias_listed[:, HALF:N], bias_row[:].indirect(offsets[:, 2 * cols : 4 * cols]))
 

@@ -26,9 +26,15 @@ HALF = N // 2
 QUARTER = N // 4
 TILES = N // P
 KB_ROW = P - 1
+LEAD = 512
+V_BIAS = 2048
 
 FLOPS = 2 * 512 * NQ * N
 BYTES = P * T * 4 + 16 * T + 4 * T + 512 * NQ * 4 + NQ * 4 + P * 64 * 2 + NQ * 32 * 4
+
+
+def runs(ap):
+    return ap.rearrange("p (j s) -> p j s", s=SEG)
 
 
 def tile_attend_xtr_kernel(tc, qT, k_words, k_scales, kb, im, offs, out):
@@ -38,44 +44,40 @@ def tile_attend_xtr_kernel(tc, qT, k_words, k_scales, kb, im, offs, out):
         shared = ctx.enter_context(tc.tile_pool(name="shared", bufs=1))
         psum = ctx.enter_context(tc.psum_pool(name="psum", bufs=1))
 
-        at_sums = 0
+        scales = keep.tile([P, T], U8, name="scales", align_bytes=64)
+        scale_words = scales[:].bitcast(I32)
+        nc.vector.memset(scale_words[:, 0:255], 0)
+        nc.vector.memset(scale_words[:, 255:512], 0)
+        nc.gpsimd.memset(scale_words[:, 512:1024], 0)
 
+        q_raw = keep.tile([P, PACK, NQ], F32, name="q_raw", align_bytes=64)
+        nc.sync.dma_start(q_raw[:], qT[0].rearrange("(p j) w -> p j w", j=PACK))
+        words = keep.tile([P, T], I32, name="words", align_bytes=64)
+        words_hbm = k_words[0].rearrange("p n t -> p (n t)").bitcast(I32)
+        nc.sync.dma_start(words[:, 0:LEAD], words_hbm[:, 0:LEAD])
         bias_row = keep.tile([P, T], F32, name="bias_row", align_bytes=64)
         nc.sync.dma_start(bias_row[KB_ROW:P, :], kb[0:1, :])
         offsets = keep.tile([P, N // 16], U16, name="offsets")
         nc.sync.dma_start(offsets[:], offs)
-        scales = keep.tile([P, T], U8, name="scales", align_bytes=64)
-        scale_words = scales[:].bitcast(I32)
-        nc.sync.dma_start(scale_words[48:64, :], k_scales[0].bitcast(I32))
-        q_raw = keep.tile([P, PACK, NQ], F32, name="q_raw", align_bytes=64)
-        nc.sync.dma_start(q_raw[:], qT[0].rearrange("(p j) w -> p j w", j=PACK))
-
-        nc.vector.memset(scale_words[0:48, 0:511], 0)
-        nc.vector.memset(scale_words[0:48, 511:1024], 0)
-        nc.gpsimd.memset(scale_words[64:P, :], 0)
+        nc.sync.dma_start(scale_words[32:96:4, :], k_scales[0].bitcast(I32))
+        nc.sync.dma_start(words[:, LEAD:T], words_hbm[:, LEAD:T])
+        floor = keep.tile([P, 1], F32, name="floor")
+        nc.sync.dma_start(floor[:], im[0])
 
         diagonal = keep.tile([P, P], F32, name="diagonal")
         nc.gpsimd.iota(diagonal[:], [[1, P]], base=0, channel_multiplier=-1, allow_small_or_imprecise_dtypes=True)
 
         bias_words = bias_row[0:KB_ROW, :].bitcast(I32)
-        nc.vector.memset(bias_words[:, 0:991], 0)
-        nc.vector.memset(bias_words[:, 991:1984], 0)
-        nc.gpsimd.memset(bias_words[:, 1984:T], 0)
+        nc.vector.memset(bias_words[:, 0 : V_BIAS // 2 - 1], 0)
+        nc.vector.memset(bias_words[:, V_BIAS // 2 - 1 : V_BIAS], 0)
+        nc.gpsimd.memset(bias_words[:, V_BIAS:T], 0)
+        plane = keep.tile([P, N], U8, name="plane", align_bytes=64)
+        nc.gpsimd.memset(plane[:].bitcast(I32), 0)
 
         distance = keep.tile([P, P], F32, name="distance")
         nc.scalar.activation(distance[:], diagonal[:], ABS)
         ident = keep.tile([P, P], F32, name="ident")
         nc.scalar.activation(ident[:], distance[:], RELU, bias=1.0, scale=-1.0)
-
-        words = keep.tile([P, T], I32, name="words", align_bytes=64)
-        words_hbm = k_words[0].rearrange("p n t -> p (n t)").bitcast(I32)
-        for c0 in range(0, T, 2048):
-            nc.sync.dma_start(words[:, c0 : c0 + 2048], words_hbm[:, c0 : c0 + 2048])
-        floor = keep.tile([P, 1], F32, name="floor")
-        nc.sync.dma_start(floor[:], im[0])
-
-        plane = keep.tile([P, N], U8, name="plane", align_bytes=64)
-        nc.gpsimd.memset(plane[:].bitcast(I32), 0)
 
         q_grouped = keep.tile([P, NQ * PACK], BF16, name="q_grouped", align_bytes=64)
         nc.scalar.activation(
@@ -86,7 +88,7 @@ def tile_attend_xtr_kernel(tc, qT, k_words, k_scales, kb, im, offs, out):
         nc.vector.tensor_copy(scales_listed[:], scales[:].indirect(offsets[:]))
         cols = QUARTER // 16
         bias_listed = keep.tile([P, N], F32, name="bias_listed", align_bytes=64)
-        for g in range(2):
+        for g in range(4):
             nc.scalar.activation(
                 bias_listed[:, g * QUARTER : (g + 1) * QUARTER],
                 bias_row[:].indirect(offsets[:, g * cols : (g + 1) * cols]),
@@ -94,15 +96,13 @@ def tile_attend_xtr_kernel(tc, qT, k_words, k_scales, kb, im, offs, out):
             )
         for r in range(4):
             queue = nc.scalar if r % 2 else nc.sync
-            queue.dma_start(plane[r:P:32, :].bitcast(I32), scales_listed[48 + r : 64 : 4, :].bitcast(I32))
-
-        nc.vector.tensor_copy(bias_listed[:, HALF:N], bias_row[:].indirect(offsets[:, 2 * cols : 4 * cols]))
+            queue.dma_start(plane[r:P:32, :].bitcast(I32), scales_listed[32 + 4 * r : 96 : 16, :].bitcast(I32))
 
         q_codes = keep.tile([P, NQ], U32, name="q_codes", align_bytes=64)
         q_scales = keep.tile([P, NQ], U8, name="q_scales", align_bytes=64)
         nc.vector.quantize_mx(out=q_codes[:].bitcast(FP8X4), scales=q_scales[:], in_=q_grouped[:])
 
-        bias_cols = shared.tile([P, TILES], F32, name="bias_cols", align_bytes=64, offset=at_sums)
+        bias_cols = shared.tile([P, TILES], F32, name="bias_cols", align_bytes=64, offset=0)
         for h in range(2):
             turned = psum.tile([P, 4, P], F32, name="turned", tag="b%d" % h)
             for i in range(4):
@@ -115,12 +115,9 @@ def tile_attend_xtr_kernel(tc, qT, k_words, k_scales, kb, im, offs, out):
             for i in range(4):
                 t = 4 * h + i
                 nc.tensor.transpose(spread[:, i, :], bias_cols[:, t : t + 1].to_broadcast([P, P]), ident[:])
-            for c0, c1 in ((0, HALF),) if h == 0 else ((0, QUARTER), (QUARTER, HALF)):
-                nc.scalar.copy(
-                    bias_wide[:, h * HALF + c0 : h * HALF + c1], spread[:].rearrange("p i n -> p (i n)")[:, c0:c1]
-                )
+            nc.scalar.copy(bias_wide[:, h * HALF : (h + 1) * HALF], spread[:].rearrange("p i n -> p (i n)"))
 
-        summed = shared.tile([P, N // SEG, SEG + 4], F32, name="summed", align_bytes=64, offset=at_sums)
+        summed = shared.tile([P, N // SEG, SEG + 4], F32, name="summed", align_bytes=64, offset=0)
         nc.scalar.copy(summed[:, :, SEG], floor[:].to_broadcast([P, N // SEG]))
 
         words_listed = keep.tile([P, N], U32, name="words_listed", align_bytes=64)
@@ -130,30 +127,28 @@ def tile_attend_xtr_kernel(tc, qT, k_words, k_scales, kb, im, offs, out):
                 words[:].bitcast(U32).indirect(offsets[:, g * cols : (g + 1) * cols]),
             )
 
-        c0 = 0
-        for width, tag in ((P, "b0"), (P, "b4"), (QUARTER, "b5"), (QUARTER, "b6"), (QUARTER, "b7")):
-            bank = psum.tile([P, width], F32, name="bank", tag=tag)
+        per = QUARTER // SEG
+        for g in range(4):
+            c0, c1 = g * QUARTER, (g + 1) * QUARTER
+            bank = psum.tile([P, QUARTER], F32, name="bank", tag="b%d" % (4 + g))
             nc.tensor.matmul_mx(
                 out=bank[:],
                 lhsT=q_codes[:].bitcast(FP8X4),
                 lhsT_scale=q_scales[:],
-                rhs=words_listed[:, c0 : c0 + width].bitcast(FP8X4),
-                rhs_scale=plane[:, c0 : c0 + width],
+                rhs=words_listed[:, c0:c1].bitcast(FP8X4),
+                rhs_scale=plane[:, c0:c1],
                 start=True,
                 stop=True,
             )
-            nc.vector.tensor_tensor(
-                summed[:, c0 // SEG : (c0 + width) // SEG, 0:SEG],
-                bank[:].rearrange("p (j s) -> p j s", s=SEG),
-                bias_wide[:, c0 : c0 + width].rearrange("p (j s) -> p j s", s=SEG),
-                ADD,
-            )
-            c0 = c0 + width
+            sums = summed[:, g * per : (g + 1) * per, 0:SEG]
+            if g == 0:
+                scores = keep.tile([P, QUARTER], F32, name="scores", align_bytes=64)
+                nc.scalar.copy(scores[:], bank[:])
+                nc.gpsimd.tensor_tensor(sums, runs(scores[:]), runs(bias_wide[:, c0:c1]), ADD)
+            else:
+                nc.vector.tensor_tensor(sums, runs(bank[:]), runs(bias_wide[:, c0:c1]), ADD)
         best = keep.tile([P, N // SEG], F32, name="best")
-        runs = HALF // SEG
-        for h in range(2):
-            nc.vector.tensor_reduce(
-                best[:, h * runs : (h + 1) * runs], summed[:, h * runs : (h + 1) * runs, 0 : SEG + 1], AXIS_X, MAX
-            )
+        for j0, j1 in ((per, 3 * per), (0, per), (3 * per, 4 * per)):
+            nc.vector.tensor_reduce(best[:, j0:j1], summed[:, j0:j1, 0 : SEG + 1], AXIS_X, MAX)
 
         nc.sync.dma_start(out[0], best[:])

@@ -115,7 +115,10 @@ def tile_attend_xtr_kernel(tc, qT, k_words, k_scales, kb, im, offs, out):
             for i in range(4):
                 t = 4 * h + i
                 nc.tensor.transpose(spread[:, i, :], bias_cols[:, t : t + 1].to_broadcast([P, P]), ident[:])
-            nc.scalar.copy(bias_wide[:, h * HALF : (h + 1) * HALF], spread[:].rearrange("p i n -> p (i n)"))
+            for c0, c1 in ((0, HALF),) if h == 0 else ((0, QUARTER), (QUARTER, HALF)):
+                nc.scalar.copy(
+                    bias_wide[:, h * HALF + c0 : h * HALF + c1], spread[:].rearrange("p i n -> p (i n)")[:, c0:c1]
+                )
 
         summed = shared.tile([P, N // SEG, SEG + 4], F32, name="summed", align_bytes=64, offset=0)
         nc.scalar.copy(summed[:, :, SEG], floor[:].to_broadcast([P, N // SEG]))
@@ -127,10 +130,10 @@ def tile_attend_xtr_kernel(tc, qT, k_words, k_scales, kb, im, offs, out):
                 words[:].bitcast(U32).indirect(offsets[:, g * cols : (g + 1) * cols]),
             )
 
-        per = QUARTER // SEG
-        for g in range(4):
-            c0, c1 = g * QUARTER, (g + 1) * QUARTER
-            bank = psum.tile([P, QUARTER], F32, name="bank", tag="b%d" % (4 + g))
+        c0 = 0
+        for width, tag in ((P, "b0"), (P, "b1"), (QUARTER, "b4"), (QUARTER, "b5"), (P, "b6"), (P, "b7")):
+            c1 = c0 + width
+            bank = psum.tile([P, width], F32, name="bank", tag=tag)
             nc.tensor.matmul_mx(
                 out=bank[:],
                 lhsT=q_codes[:].bitcast(FP8X4),
@@ -140,15 +143,18 @@ def tile_attend_xtr_kernel(tc, qT, k_words, k_scales, kb, im, offs, out):
                 start=True,
                 stop=True,
             )
-            sums = summed[:, g * per : (g + 1) * per, 0:SEG]
-            if g == 0:
-                scores = keep.tile([P, QUARTER], F32, name="scores", align_bytes=64)
+            sums = summed[:, c0 // SEG : c1 // SEG, 0:SEG]
+            if c1 == N:
+                scores = keep.tile([P, width], F32, name="scores", align_bytes=64)
                 nc.scalar.copy(scores[:], bank[:])
                 nc.gpsimd.tensor_tensor(sums, runs(scores[:]), runs(bias_wide[:, c0:c1]), ADD)
             else:
                 nc.vector.tensor_tensor(sums, runs(bank[:]), runs(bias_wide[:, c0:c1]), ADD)
+            c0 = c1
         best = keep.tile([P, N // SEG], F32, name="best")
-        for j0, j1 in ((per, 3 * per), (0, per), (3 * per, 4 * per)):
-            nc.vector.tensor_reduce(best[:, j0:j1], summed[:, j0:j1, 0 : SEG + 1], AXIS_X, MAX)
+        for c0, c1 in ((0, HALF), (HALF, N - P), (N - P, N)):
+            nc.vector.tensor_reduce(
+                best[:, c0 // SEG : c1 // SEG], summed[:, c0 // SEG : c1 // SEG, 0 : SEG + 1], AXIS_X, MAX
+            )
 
         nc.sync.dma_start(out[0], best[:])

@@ -27,7 +27,7 @@ QUARTER = N // 4
 TILES = N // P
 KB_ROW = P - 1
 LEAD = 512
-V_BIAS = 2048
+V_BIAS = 2304
 
 FLOPS = 2 * 512 * NQ * N
 BYTES = P * T * 4 + 16 * T + 4 * T + 512 * NQ * 4 + NQ * 4 + P * 64 * 2 + NQ * 32 * 4
@@ -59,7 +59,7 @@ def tile_attend_xtr_kernel(tc, qT, k_words, k_scales, kb, im, offs, out):
         nc.sync.dma_start(bias_row[KB_ROW:P, :], kb[0:1, :])
         offsets = keep.tile([P, N // 16], U16, name="offsets")
         nc.sync.dma_start(offsets[:], offs)
-        nc.sync.dma_start(scale_words[32:96:4, :], k_scales[0].bitcast(I32))
+        nc.sync.dma_start(scale_words[0:P:8, :], k_scales[0].bitcast(I32))
         nc.sync.dma_start(words[:, LEAD:T], words_hbm[:, LEAD:T])
         floor = keep.tile([P, 1], F32, name="floor")
         nc.sync.dma_start(floor[:], im[0])
@@ -71,8 +71,6 @@ def tile_attend_xtr_kernel(tc, qT, k_words, k_scales, kb, im, offs, out):
         nc.vector.memset(bias_words[:, 0 : V_BIAS // 2 - 1], 0)
         nc.vector.memset(bias_words[:, V_BIAS // 2 - 1 : V_BIAS], 0)
         nc.gpsimd.memset(bias_words[:, V_BIAS:T], 0)
-        plane = keep.tile([P, N], U8, name="plane", align_bytes=64)
-        nc.gpsimd.memset(plane[:].bitcast(I32), 0)
 
         distance = keep.tile([P, P], F32, name="distance")
         nc.scalar.activation(distance[:], diagonal[:], ABS)
@@ -94,9 +92,11 @@ def tile_attend_xtr_kernel(tc, qT, k_words, k_scales, kb, im, offs, out):
                 bias_row[:].indirect(offsets[:, g * cols : (g + 1) * cols]),
                 COPY,
             )
-        for r in range(4):
+        plane = keep.tile([P, N], U8, name="plane", align_bytes=64)
+        nc.vector.tensor_copy(plane[:].bitcast(I32), scales_listed[:].bitcast(I32))
+        for r in range(1, 4):
             queue = nc.scalar if r % 2 else nc.sync
-            queue.dma_start(plane[r:P:32, :].bitcast(I32), scales_listed[32 + 4 * r : 96 : 16, :].bitcast(I32))
+            queue.dma_start(plane[r:P:32, :].bitcast(I32), scales_listed[8 * r : P : 32, :].bitcast(I32))
 
         q_codes = keep.tile([P, NQ], U32, name="q_codes", align_bytes=64)
         q_scales = keep.tile([P, NQ], U8, name="q_scales", align_bytes=64)

from contextlib import ExitStack

import concourse.mybir as mybir

F32 = mybir.dt.float32
BF16 = mybir.dt.bfloat16
I32 = mybir.dt.int32
U32 = mybir.dt.uint32
U16 = mybir.dt.uint16
U8 = mybir.dt.uint8
FP8X4 = mybir.dt.float8_e4m3fn_x4
COPY = mybir.ActivationFunctionType.Copy
ABS = mybir.ActivationFunctionType.Abs
RELU = mybir.ActivationFunctionType.Relu
MAX = mybir.AluOpType.max
ADD = mybir.AluOpType.add
AXIS_X = mybir.AxisListType.X

P = 128
PACK = 4
T = 4096
N = 1024
NQ = 128
SEG = 32
HALF = N // 2
QUARTER = N // 4
TILES = N // P
KB_ROW = P - 1
LEAD = 512
V_BIAS = 2304

FLOPS = 2 * 512 * NQ * N
BYTES = P * T * 4 + 16 * T + 4 * T + 512 * NQ * 4 + NQ * 4 + P * 64 * 2 + NQ * 32 * 4


def runs(ap):
    return ap.rearrange("p (j s) -> p j s", s=SEG)


def tile_attend_xtr_kernel(tc, qT, k_words, k_scales, kb, im, offs, out):
    nc = tc.nc
    with ExitStack() as ctx:
        keep = ctx.enter_context(tc.tile_pool(name="keep", bufs=1))
        shared = ctx.enter_context(tc.tile_pool(name="shared", bufs=1))
        psum = ctx.enter_context(tc.psum_pool(name="psum", bufs=1))

        scales = keep.tile([P, T], U8, name="scales", align_bytes=64)
        scale_words = scales[:].bitcast(I32)
        nc.vector.memset(scale_words[:, 0:255], 0)
        nc.vector.memset(scale_words[:, 255:512], 0)
        nc.gpsimd.memset(scale_words[:, 512:1024], 0)

        q_raw = keep.tile([P, PACK, NQ], F32, name="q_raw", align_bytes=64)
        nc.sync.dma_start(q_raw[:], qT[0].rearrange("(p j) w -> p j w", j=PACK))
        words = keep.tile([P, T], I32, name="words", align_bytes=64)
        words_hbm = k_words[0].rearrange("p n t -> p (n t)").bitcast(I32)
        nc.sync.dma_start(words[:, 0:LEAD], words_hbm[:, 0:LEAD])
        bias_row = keep.tile([P, T], F32, name="bias_row", align_bytes=64)
        nc.sync.dma_start(bias_row[KB_ROW:P, :], kb[0:1, :])
        offsets = keep.tile([P, N // 16], U16, name="offsets")
        nc.sync.dma_start(offsets[:], offs)
        nc.sync.dma_start(scale_words[0:P:8, :], k_scales[0].bitcast(I32))
        nc.sync.dma_start(words[:, LEAD:T], words_hbm[:, LEAD:T])
        floor = keep.tile([P, 1], F32, name="floor")
        nc.sync.dma_start(floor[:], im[0])

        diagonal = keep.tile([P, P], F32, name="diagonal")
        nc.gpsimd.iota(diagonal[:], [[1, P]], base=0, channel_multiplier=-1, allow_small_or_imprecise_dtypes=True)

        bias_words = bias_row[0:KB_ROW, :].bitcast(I32)
        nc.vector.memset(bias_words[:, 0 : V_BIAS // 2 - 1], 0)
        nc.vector.memset(bias_words[:, V_BIAS // 2 - 1 : V_BIAS], 0)
        nc.gpsimd.memset(bias_words[:, V_BIAS:T], 0)

        distance = keep.tile([P, P], F32, name="distance")
        nc.scalar.activation(distance[:], diagonal[:], ABS)
        ident = keep.tile([P, P], F32, name="ident")
        nc.scalar.activation(ident[:], distance[:], RELU, bias=1.0, scale=-1.0)

        q_grouped = keep.tile([P, NQ * PACK], BF16, name="q_grouped", align_bytes=64)
        nc.scalar.activation(
            q_grouped[:].rearrange("p (w j) -> p w j", j=PACK), q_raw[:].rearrange("p j w -> p w j"), COPY
        )

        scales_listed = keep.tile([P, N], U8, name="scales_listed", align_bytes=64)
        nc.vector.tensor_copy(scales_listed[:], scales[:].indirect(offsets[:]))
        cols = QUARTER // 16
        bias_listed = keep.tile([P, N], F32, name="bias_listed", align_bytes=64)
        for g in range(4):
            nc.scalar.activation(
                bias_listed[:, g * QUARTER : (g + 1) * QUARTER],
                bias_row[:].indirect(offsets[:, g * cols : (g + 1) * cols]),
                COPY,
            )
        plane = keep.tile([P, N], U8, name="plane", align_bytes=64)
        nc.vector.tensor_copy(plane[:].bitcast(I32), scales_listed[:].bitcast(I32))
        for r in range(1, 4):
            queue = nc.scalar if r % 2 else nc.sync
            queue.dma_start(plane[r:P:32, :].bitcast(I32), scales_listed[8 * r : P : 32, :].bitcast(I32))

        q_codes = keep.tile([P, NQ], U32, name="q_codes", align_bytes=64)
        q_scales = keep.tile([P, NQ], U8, name="q_scales", align_bytes=64)
        nc.vector.quantize_mx(out=q_codes[:].bitcast(FP8X4), scales=q_scales[:], in_=q_grouped[:])

        bias_cols = shared.tile([P, TILES], F32, name="bias_cols", align_bytes=64, offset=0)
        for h in range(2):
            turned = psum.tile([P, 4, P], F32, name="turned", tag="b%d" % h)
            for i in range(4):
                t = 4 * h + i
                nc.tensor.transpose(turned[:, i, :], bias_listed[:, t * P : (t + 1) * P], ident[:])
            nc.scalar.copy(bias_cols[:, 4 * h : 4 * h + 4], turned[:, :, KB_ROW])
        bias_wide = keep.tile([P, N], F32, name="bias_wide")
        for h in range(2):
            spread = psum.tile([P, 4, P], F32, name="spread", tag="b%d" % (2 + h))
            for i in range(4):
                t = 4 * h + i
                nc.tensor.transpose(spread[:, i, :], bias_cols[:, t : t + 1].to_broadcast([P, P]), ident[:])
            for c0, c1 in ((0, HALF),) if h == 0 else ((0, QUARTER), (QUARTER, HALF)):
                nc.scalar.copy(
                    bias_wide[:, h * HALF + c0 : h * HALF + c1], spread[:].rearrange("p i n -> p (i n)")[:, c0:c1]
                )

        summed = shared.tile([P, N // SEG, SEG + 4], F32, name="summed", align_bytes=64, offset=0)
        nc.scalar.copy(summed[:, :, SEG], floor[:].to_broadcast([P, N // SEG]))

        words_listed = keep.tile([P, N], U32, name="words_listed", align_bytes=64)
        for g in range(4):
            nc.vector.tensor_copy(
                words_listed[:, g * QUARTER : (g + 1) * QUARTER],
                words[:].bitcast(U32).indirect(offsets[:, g * cols : (g + 1) * cols]),
            )

        c0 = 0
        for width, tag in ((P, "b0"), (P, "b1"), (QUARTER, "b4"), (QUARTER, "b5"), (P, "b6"), (P, "b7")):
            c1 = c0 + width
            bank = psum.tile([P, width], F32, name="bank", tag=tag)
            nc.tensor.matmul_mx(
                out=bank[:],
                lhsT=q_codes[:].bitcast(FP8X4),
                lhsT_scale=q_scales[:],
                rhs=words_listed[:, c0:c1].bitcast(FP8X4),
                rhs_scale=plane[:, c0:c1],
                start=True,
                stop=True,
            )
            sums = summed[:, c0 // SEG : c1 // SEG, 0:SEG]
            if c1 == N:
                scores = keep.tile([P, width], F32, name="scores", align_bytes=64)
                nc.scalar.copy(scores[:], bank[:])
                nc.gpsimd.tensor_tensor(sums, runs(scores[:]), runs(bias_wide[:, c0:c1]), ADD)
            else:
                nc.vector.tensor_tensor(sums, runs(bank[:]), runs(bias_wide[:, c0:c1]), ADD)
            c0 = c1
        best = keep.tile([P, N // SEG], F32, name="best")
        for c0, c1 in ((0, HALF), (HALF, N - P), (N - P, N)):
            nc.vector.tensor_reduce(
                best[:, c0 // SEG : c1 // SEG], summed[:, c0 // SEG : c1 // SEG, 0 : SEG + 1], AXIS_X, MAX
            )

        nc.sync.dma_start(out[0], best[:])
